import numpy as np, ml_dtypes
CORES = [113,118,241,246]
N = 4
BF = ml_dtypes.bfloat16
def gentries(a):
    return np.ascontiguousarray(a.reshape(8, 16, -1).transpose(0, 2, 1)).reshape(8, -1)
def gtable(e):
    e = np.asarray(e); return np.ascontiguousarray(e.reshape(8, -1, 16).transpose(0, 2, 1)).reshape(128, -1).astype(np.int32)
BASE, K, E, CL, RO = 2560, 1024, 1024, 2, 4
W = BASE + 2 * K
def injections(rng, share):
    v = np.argsort(rng.random((N, 8, W, 16), dtype=np.float32), axis=3)
    return np.where(rng.random((N, 8, W, 16), dtype=np.float32) < share, -1, v)
def parts(rng, v):
    return {"idm": v, "par": rng.integers(0, W, (N, 8, W)), "mnt": rng.integers(0, W, (N, 8, E)), "ac": rng.integers(0, E, (N, 8, 16, E)),
            "ns0": rng.integers(0, W, (N, 8, K)), "u0": rng.integers(0, 16, (N, 8, K)), "e0": rng.integers(0, E, (N, 8, K))}
def pack(d):
    return {"idm": np.ascontiguousarray(d["idm"].transpose(0, 1, 3, 2).reshape(N, 128, W)).astype(np.float32).astype(BF), "par": d["par"].astype(np.int32), "mnt": d["mnt"].astype(np.int32),
            "ac": np.ascontiguousarray(d["ac"].reshape(N, 128, E)).astype(np.int32), "ns0": np.stack([gtable(a) for a in d["ns0"]]), "u0": d["u0"].astype(np.int32), "e0": np.stack([gtable(a) for a in d["e0"]])}
def setup_inputs(rng):
    return pack(parts(rng, injections(rng, rng.choice(np.array([0.03125, 0.0625, 0.125, 0.25]), (N, 8, W, 1)))))
def skew(rng, hi, shape):
    v = np.minimum((hi * rng.random(shape) ** 3).astype(np.int64), hi - 1); s = rng.random(shape[:2] + (1,) * (len(shape) - 2)) < 0.5
    return np.where(s, v, hi - 1 - v)
def setup_inputs_spread(rng):
    return pack({"idm": injections(rng, 0.5 * rng.random((N, 8, W, 1)) ** 2), "par": skew(rng, W, (N, 8, W)), "mnt": skew(rng, W, (N, 8, E)), "ac": skew(rng, E, (N, 8, 16, E)),
                 "ns0": skew(rng, W, (N, 8, K)), "u0": skew(rng, 16, (N, 8, K)), "e0": skew(rng, E, (N, 8, K))})
def atends(rng, hi, shape):
    return np.where(rng.random(shape) < 0.8, (hi - 1) * rng.integers(0, 2, shape), rng.integers(0, hi, shape))
def setup_inputs_ends(rng):
    full = injections(rng, 0.0625); sp = np.full((N, 8, W, 16), -1); z = rng.random((N, 8, W)) < 0.75
    sp[..., 15] = np.where(z, 15, -1); sp[..., 0] = np.where(z, -1, 15)
    v = np.where(rng.random((N, 8, W, 1)) < 0.7, sp, full)
    mid = np.argsort(rng.random((N, 8, 2, 14)), axis=3) + 1
    v[:, :, [0, W - 1], 1:15] = np.where(rng.random(mid.shape) < 0.125, -1, mid); v[:, :, [0, W - 1], 0] = 0; v[:, :, [0, W - 1], 15] = 15
    d = {"idm": v, "par": atends(rng, W, (N, 8, W)), "mnt": atends(rng, W, (N, 8, E)), "ac": atends(rng, E, (N, 8, 16, E)),
         "ns0": atends(rng, W, (N, 8, K)), "u0": atends(rng, 16, (N, 8, K)), "e0": atends(rng, E, (N, 8, K))}
    d["par"][:, :, 0] = 0; d["par"][:, :, W - 1] = W - 1; d["mnt"][:, :, 0] = 0; d["mnt"][:, :, E - 1] = W - 1; d["ac"][:, :, 0, 0] = 0; d["ac"][:, :, 15, E - 1] = E - 1
    x = rng.random((N, 8, K)); top = x < 0.125; low = x > 0.875
    top[..., [1, 2, K - 1]] = True; low[..., [1, 2, K - 1]] = False; top[..., 0] = False; low[..., 0] = True
    for k, hi in (("ns0", W - 1), ("u0", 15), ("e0", E - 1)): d[k] = np.where(top, hi, np.where(low, 0, d[k]))
    return pack(d)
def setup_inputs_corners(rng):
    full = injections(rng, 0.0); v = np.where(rng.random(full.shape, dtype=np.float32) < 0.0625, -1, full); d = parts(rng, v); num = np.arange(W); row = np.arange(16)
    for r in range(N):
        for g in range(8):
            s = (g + 3 * r) % 8
            if s == 0:
                c = rng.integers(0, 3, (W, 1)); v[r, g] = np.where(c == 0, -1, np.where(c == 1, row, full[r, g]))
            if s == 1:
                one = row == rng.integers(0, 16, (W, 1)); v[r, g] = np.where(one | (rng.random((W, 1)) < 0.5), full[r, g], -1)
            if s in (2, 3, 4): v[r, g] = full[r, g]; d["par"][r, g] = (num, 0 * num, 0 * num + W - 1)[s - 2]
            if s == 5: d["par"][r, g] = np.maximum(num - 1, 0)
            if s == 6: d["par"][r, g] = rng.integers(BASE, W, W); d["mnt"][r, g] = rng.integers(BASE, W, E)
            if s == 7:
                hc = rng.permutation(BASE)[:64]; v[r, g, hc] = -1
                d["mnt"][r, g] = np.where((rng.random(E) < 0.0625) & (r % 2 == 0), d["mnt"][r, g], hc[rng.integers(0, 64, E)])
    z = rng.random((N, 8, K)); own = BASE + K * rng.integers(0, 2, (N, 8, K)) + np.arange(K); edge = rng.choice(np.array([0, W - 1, BASE - 1, BASE, BASE + K - 1, BASE + K]), (N, 8, K))
    d["ns0"] = np.where(z < 0.25, own, np.where(z < 0.5, edge, d["ns0"])); d["u0"] = np.where(rng.random((N, 8, K)) < 0.5, 15 * rng.integers(0, 2, (N, 8, K)), d["u0"])
    return pack(d)
def setup_inputs_alike(rng):
    d = parts(rng, injections(rng, 0.0625))
    for r in range(N):
        for g in range(8):
            s = (g + r) % 4
            for k, hi in (("ns0", W), ("e0", E)):
                old = d[k][r, g].copy(); few = rng.integers(0, hi, 4)
                if s < 2: d[k][r, g] = few[0]
                if s == 1: d[k][r, g, K - 1 - r] = old[K - 1 - r]
                if s == 2: d[k][r, g] = few[rng.integers(0, 4, K)]
            if s == 0: d["u0"][r, g] = rng.integers(0, 16)
        d["ac"][r, 2] = rng.integers(0, E); d["mnt"][r, 4] = rng.integers(0, W); d["par"][r, 6] = rng.integers(0, W)
    d["ac"][:, 1::2] = rng.choice(np.array([0, E - 1, E // 2, 3]), (N, 4, 16, E)); d["mnt"][:, 5] = rng.choice(np.array([0, W - 1, BASE, BASE + K]), (N, E))
    return pack(d)
def setup_inputs_calm(rng):
    v = (np.argsort(rng.random((N, 8, W, 4, 4), dtype=np.float32), axis=4) + 4 * np.arange(4)[:, None]).reshape(N, 8, W, 16)
    d = parts(rng, np.where(rng.random(v.shape, dtype=np.float32) < 0.05, -1, v))
    for g in range(8):
        h = (g + 1) % 8
        if g % 2 == 0:
            d["ns0"][:, g] = rng.integers(0, 4, (N, K)); d["u0"][:, g] = rng.integers(0, 4, (N, K)); d["e0"][:, g] = rng.integers(0, 4, (N, K)); d["par"][:, g] = rng.integers(0, 4, (N, W))
            d["ac"][:, h] = rng.integers(0, 4, (N, 16, E)); d["mnt"][:, h] = rng.choice(np.array([0, 1, 2, 3, BASE, BASE + 1, BASE + K, BASE + K + 1]), (N, E))
        else:
            d["ns0"][:, g] = W - 1 - rng.integers(0, 2, (N, K)); d["u0"][:, g] = 15 - rng.integers(0, 2, (N, K)); d["e0"][:, g] = E - 1 - rng.integers(0, 2, (N, K)); d["par"][:, g] = W - 1 - rng.integers(0, 2, (N, W))
            d["ac"][:, h] = E - 1 - rng.integers(0, 2, (N, 16, E)); d["mnt"][:, h] = rng.choice(np.array([W - 1, W - 2, BASE + K - 1, BASE + K - 2, BASE - 1, BASE - 2]), (N, E))
    return pack(d)
def check_inputs(d):
    bad = []
    for k, lo, hi in (("idm", -1, 15), ("par", 0, W - 1), ("mnt", 0, W - 1), ("ac", 0, E - 1), ("ns0", 0, W - 1), ("u0", 0, 15), ("e0", 0, E - 1)):
        v = np.asarray(d[k]).astype(np.float64)
        if not (np.min(v) >= lo and np.max(v) <= hi): bad.append("range of " + k)
    v = np.asarray(d["idm"]).astype(np.float32)
    if not np.all(v == np.rint(v)): bad.append("whole numbers in idm")
    s = np.sort(v.reshape(-1, 8, 16, W), axis=2)
    if np.any((s[:, :, 1:] == s[:, :, :-1]) & (s[:, :, 1:] >= 0)): bad.append("an id twice in a column of idm")
    return bad
def reference(idm, par, mnt, ac, ns0, u0, e0):
    a = np.ascontiguousarray(idm.astype(np.float32).astype(np.int64).reshape(N, 8, 16, W).transpose(0, 1, 3, 2))
    p = par.astype(np.int64); mt = mnt.astype(np.int64); mv = ac.astype(np.int64).reshape(N, 8, 16, E)
    ns = np.stack([gentries(x) for x in ns0]).astype(np.int64); e = np.stack([gentries(x) for x in e0]).astype(np.int64); u = u0.astype(np.int64)
    R = np.arange(N)[:, None, None]; G = np.arange(8)[None, :, None]; H = (G + 1) % 8
    for t in range(RO):
        w = u; n = ns
        for step in range(CL):
            w = np.where(w >= 0, a[R, G, n, np.maximum(w, 0)], -1); n = p[R, G, n]
        Q = (R + 1 + t % (N - 1)) % N
        col = a[Q, H, mt[Q, H, e]]
        hit = (col == w[..., None]) & (w[..., None] >= 0); ok = np.any(hit, axis=3); k = np.argmax(hit, axis=3)
        e2 = mv[Q, H, k, e]; up = p[R, G, ns]; S = BASE + K * (t % 2)
        if t < RO - 1:
            a[:, :, S:S + K] = np.where(ok[..., None], col, a[:, :, S:S + K]); p[:, :, S:S + K] = np.where(ok, ns, p[:, :, S:S + K])
        ns = np.where(ok, S + e2 % K, up); u = np.where(ok, k, u); e = np.where(ok, e2, e)
    return {"yn": np.stack([gtable(x) for x in ns]).astype(np.float32), "yu": u.astype(np.float32), "ye": np.stack([gtable(x) for x in e]).astype(np.float32)}

@@ -1,0 +1,463 @@
+from concourse.mybir import AluOpType, ActivationFunctionType
+
+A = AluOpType
+F = ActivationFunctionType
+BASE, K, W, RO = 2560, 1024, 4608, 4
+DELTA = [0.75, 0.5, 0.25, 0.125]
+BIG = 8192
+
+SCRATCH = {
+    "tab": ("sbuf", [128, W], "bfloat16"),
+    "part": ("sbuf", [128, W], "bfloat16"),
+    "parb": ("sbuf", [128, 288], "int32"),
+    "parh": ("sbuf", [128, 288], "bfloat16"),
+    "parl": ("sbuf", [128, 288], "bfloat16"),
+    "rows": ("sbuf", [16, K], "int32"),
+    "rowf": ("sbuf", [16, K], "float32"),
+    "rowb": ("sbuf", [16, K], "bfloat16"),
+    "acs": ("sbuf", [128, K], "int32"),
+    "acu": ("sbuf", [128, K], "uint16"),
+    "acl": ("sbuf", [128, K], "uint16"),
+    "ac0": ("sbuf", [128, K], "int32"),
+    "ac1": ("sbuf", [128, K], "int32"),
+    "ac2": ("sbuf", [128, K], "int32"),
+    "x": ("sbuf", [128, K], "bfloat16"),
+    "y1": ("sbuf", [128, K], "bfloat16"),
+    "p1": ("sbuf", [128, K], "bfloat16"),
+    "m1": ("sbuf", [128, K], "bfloat16"),
+    "y2": ("sbuf", [128, K], "bfloat16"),
+    "z": ("sbuf", [128, K], "bfloat16"),
+    "mk": ("sbuf", [128, K], "bfloat16"),
+    "r1": ("sbuf", [128, K], "bfloat16"),
+    "y3": ("sbuf", [128, K], "float16"),
+    "moff": ("sbuf", [128, 64], "uint16"),
+    "n1off": ("sbuf", [128, 64], "uint16"),
+    "uoff": ("sbuf", [128, 64], "uint16"),
+    "us": ("sbuf", [128, 64], "int32"),
+    "um": ("sbuf", [128, 64], "int32"),
+    "ub": ("sbuf", [128, 64], "int32"),
+    "up": ("sbuf", [128, 64], "int32"),
+    "op0": ("sbuf", [128, 64], "float32"),
+    "op1": ("sbuf", [128, 64], "float32"),
+    "op2": ("sbuf", [128, 64], "float32"),
+    "pnx": ("sbuf", [128, 64], "float32"),
+    "dn": ("sbuf", [128, 64], "float32"),
+    "okf": ("sbuf", [128, 64], "float32"),
+    "tq": ("sbuf", [128, 64], "float32"),
+    "pnh": ("sbuf", [128, 64], "bfloat16"),
+    "pnl": ("sbuf", [128, 64], "bfloat16"),
+    "mn": ("sbuf", [128, 64], "int32"),
+    "me": ("sbuf", [128, 64], "int32"),
+    "ns": ("sbuf", [128, 64], "int32"),
+    "ev": ("sbuf", [128, 64], "int32"),
+    "noff": ("sbuf", [128, 64], "uint16"),
+    "eoff": ("sbuf", [128, 64], "uint16"),
+    "finn": ("sbuf", [128, 64], "float32"),
+    "fine": ("sbuf", [128, 64], "float32"),
+    "finu": ("sbuf", [128, 64], "float32"),
+    "ip": ("sbuf", [128, 8], "int32"),
+    "ip2": ("sbuf", [128, 8], "int32"),
+    "cols": ("sbuf", [128, 8], "float32"),
+    "ia": ("sbuf", [128, 160], "int32"),
+    "ib": ("sbuf", [128, 160], "int32"),
+    "ia2": ("sbuf", [128, 160], "int32"),
+    "ib2": ("sbuf", [128, 160], "int32"),
+    "ic": ("sbuf", [128, 16, 8], "int32"),
+    "iv": ("sbuf", [128, 16], "int32"),
+    "iz": ("sbuf", [16, 144], "int32"),
+    "zm": ("sbuf", [16, 144], "float32"),
+    "zu": ("sbuf", [16, 144], "bfloat16"),
+    "bw": ("sbuf", [128, 160], "bfloat16"),
+    "bp": ("sbuf", [128, 160], "bfloat16"),
+    "bm": ("sbuf", [128, 160], "bfloat16"),
+    "iw": ("sbuf", [128, 160], "bfloat16"),
+    "zw": ("sbuf", [128, 160], "bfloat16"),
+    "zk": ("sbuf", [128, 160], "bfloat16"),
+    "za0": ("sbuf", [128, 160], "bfloat16"),
+    "za1": ("sbuf", [128, 160], "bfloat16"),
+    "ze": ("sbuf", [128, 160], "bfloat16"),
+    "oh": ("sbuf", [128, 16], "bfloat16"),
+    "ee": ("sbuf", [128, 16, 130], "bfloat16"),
+}
+for _t in range(RO):
+    SCRATCH["ms%d" % _t] = ("sbuf", [128, K], "bfloat16")
+    SCRATCH["ml%d" % _t] = ("sbuf", [128, K], "bfloat16")
+for _b in range(8):
+    SCRATCH["pb%d" % _b] = ("psum", [128, 512], "float32")
+
+PC = 128
+DMAS = ["idm", "mnt", "u0", "ac", "acp", "par", "ns0", "e0a", "e0b", "ph", "plo", "yn", "yea", "yeb", "yu"]
+SEMAPHORES = (["cv", "cs", "cp", "cg", "ls", "aa0", "aa1", "aa2", "aap"] + ["d_" + n for n in DMAS]
+              + ["am%d%d" % (t, h) for t in range(RO) for h in range(2)])
+
+
+def rank_program(g, core, T, topo):
+    rank = T.rank_of(core)
+    if rank is None:
+        return
+    cores = list(T.cores)
+    N = len(cores)
+    Q = {"v": g.vector, "s": g.scalar, "p": g.tensor, "g": g, "y": g.sync}
+    CN = {"v": "cv", "s": "cs", "p": "cp", "g": "cg"}
+    cnt = {}
+    known = {e: {} for e in Q}
+    lastw, readers = {}, {}
+
+    def need(e, tok):
+        sem, val, clock, _ = tok
+        if known[e].get(sem, 0) < val:
+            Q[e].wait_ge(T.sem[sem], val)
+            known[e][sem] = val
+        for s, v in clock.items():
+            if known[e].get(s, 0) < v:
+                known[e][s] = v
+
+    def deps(e, r, w, x):
+        toks = []
+        for k in list(r) + list(w) + list(x):
+            if k in lastw and not (e == "p" and lastw[k][3] == "p"):
+                toks.append(lastw[k])
+        for k in w:
+            toks += [tok for tok in readers.get(k, []) if not (e == "p" and tok[3] == "p")]
+        for k in x:
+            toks += [tok for tok in readers.get(k, []) if tok[3] != e]
+        for tok in sorted(toks, key=lambda tk: -tk[1]):
+            need(e, tok)
+
+    def note(tok, r, w, x):
+        for k in list(r) + list(x):
+            readers.setdefault(k, []).append(tok)
+        for k in w:
+            lastw[k] = tok
+            readers[k] = []
+
+    def op(e, fn, r=(), w=(), x=()):
+        deps(e, r, w, x)
+        ins = fn()
+        c = CN[e]
+        cnt[c] = cnt.get(c, 0) + 1
+        ins.then_inc(T.sem[c], 1)
+        note((c, cnt[c], dict(known[e]), e), r, w, x)
+
+    def dma(e, name, out, in_, r=(), w=()):
+        deps(e, r, w, ())
+        Q[e].dma_start(out, in_).then_inc(T.sem["d_" + name], 16)
+        cnt["d_" + name] = 16
+        note(("d_" + name, 16, dict(known[e]), "dma"), r, w, ())
+
+    def bits(engs):
+        return sum(1 << i for i in engs)
+
+    def same_chip(a, b):
+        return cores[b] in topo.cores_of(cores[a])
+
+    def lanes(src, dst, spare):
+        full = topo.engines(cores[src], cores[dst])
+        if spare and same_chip(src, dst):
+            far = [d for d in range(N) if not same_chip(src, d)][0]
+            off = topo.engines(cores[src], cores[far])
+            return [i for i in full if i not in off]
+        return full
+
+    def send(dst, out, in_, sem, r, spare):
+        deps("g", r, (), ())
+        rid, pid = topo.addr(cores[dst], core)
+        en = lanes(rank, dst, spare)
+        g.remote_dma(out, in_, T.sem[sem], T.sem.ls, pid, rid, bits(en))
+        cnt["ls"] = cnt.get("ls", 0) + len(en)
+
+    def arrives(key, sem, src, spare):
+        n = len(lanes(src, rank, spare))
+        cnt[sem] = n
+        lastw[key] = (sem, n, {}, "rem")
+
+    def mm(items, r, w):
+        def fn():
+            ins = None
+            for (o, l, rh, st, sp) in items:
+                ins = g.tensor.matmul(o, l, rh, st, sp)
+            return ins
+        op("p", fn, r=r, w=w)
+
+    def extract(out, wt, off, src, first, last, r, w, block=False, np_=128):
+        it = []
+        for k in range(16):
+            rh = src[0:np_, 64 * k:64 * k + 64] if block else src[0:np_, k:K:16]
+            it.append((out, wt[0:np_, off - k:off - k + 128], rh, first and k == 0, last and k == 15))
+        mm(it, r, w)
+
+    V, S = g.vector, g.scalar
+    pb = [T["pb%d" % b] for b in range(8)]
+    H = [slice(0, 512), slice(512, 1024)]
+    L = [slice(0, 32), slice(32, 64)]
+    TABK = ["tab", "t00", "t01", "t10", "t11"]
+    PARK = ["par", "parx", "q00", "q01", "q10", "q11"]
+    src_of = [(rank + 1 + t % 3) % N for t in range(RO)]
+    dst_of = [(rank - 1 - t % 3) % N for t in range(RO)]
+    far0 = not same_chip(rank, dst_of[0])
+    far0_in = not same_chip(rank, src_of[0])
+
+    def ts(out, in0, s1, s2, o0, o1=None, r=(), w=(), x=()):
+        if o1 is None:
+            op("v", lambda: V.tensor_scalar(out, in0, s1, None, o0), r, w, x)
+        else:
+            op("v", lambda: V.tensor_scalar(out, in0, s1, s2, o0, o1), r, w, x)
+
+    def tt(out, in0, in1, o, r=(), w=(), x=()):
+        op("v", lambda: V.tensor_tensor(out, in0, in1, o), r, w, x)
+
+    def cp(out, in_, r=(), w=(), x=()):
+        op("v", lambda: V.tensor_copy(out, in_), r, w, x)
+
+    def act(out, in_, f, r=(), w=(), x=(), **kw):
+        op("s", lambda: S.activation(out, in_, f, **kw), r, w, x)
+
+    def ac_sender(q, t):
+        d = (q - 1 - t) % N
+        if same_chip(q, d):
+            return q
+        first = [(q - 1 - s) % N for s in range(3) if not same_chip(q, (q - 1 - s) % N)][0]
+        return q if first == d else first
+
+    for t in range(RO):
+        for h in range(2):
+            arrives("ml%d%d" % (t, h), "am%d%d" % (t, h), src_of[t], False)
+    for t in range(3):
+        arrives("acl" if (t == 0 and far0_in) else "ac%d" % t, "aa%d" % t, ac_sender(src_of[t], t), True)
+
+    arrives("ac0p", "aap", src_of[0], False)
+
+    dma("s", "mnt", T.rows[0:8, :], T.mnt[:], w=["rows0"])
+    dma("y", "u0", T.rows[8:16, :], T.u0[:], w=["rows1"])
+    dma("s", "par", T.parb[:], T.par[:], w=["parb"])
+    dma("y", "acp", T.acs[:, 0:PC], T.ac[:, 0:PC], w=["acsp"])
+    dma("y", "idm", T.tab[:], T.idm[:], w=TABK)
+    dma("s", "ns0", T.ns[:], T.ns0[:], w=["ns"])
+    dma("s", "e0a", T.ev[16:128, :], T.e0[0:112, :], w=["ev"])
+    dma("s", "e0b", T.ev[0:16, :], T.e0[112:128, :], w=["ev2"])
+
+    op("g", lambda: g.iota(T.iz[:], [[1, 144]], -16, -16), w=["iz"])
+    op("g", lambda: g.iota(T.ip[:, 0:1], [[1, 1]], 0, 1), w=["ip"])
+    op("g", lambda: g.iota(T.ia[:], [[1, 160]], 112, 0), w=["ia"])
+    op("g", lambda: g.iota(T.iv[:], [[1, 16]], 0, 0), w=["iv"])
+    op("g", lambda: g.iota(T.ib[:], [[1, 160]], 128, -1), w=["ib"])
+    op("g", lambda: g.iota(T.ic[:], [[-1, 16], [-16, 8]], 0, 1), w=["ic"])
+    send(dst_of[0], T.ac0[:, 0:PC], T.acs[:, 0:PC], "aap", ["acsp"], False)
+
+    op("v", lambda: V.memset(T.part[:], 0.0), w=PARK)
+    ts(T.zm[:], T.iz[:], 0.0, None, A.is_equal, r=["iz"], w=["zm"])
+    cp(T.rowf[:], T.rows[:], r=["rows0", "rows1"], w=["rowf"])
+    extract(pb[6][:, 0:64], T.zm, 16, T.rowf, True, True, ["zm", "rowf"], ["b6"], np_=16)
+    act(T.rowb[:], T.rowf[:], F.Copy, r=["rowf"], w=["rowb"])
+    ts(T.zu[:], T.iz[:], -128.0, 512.0, A.is_equal, A.mult, r=["iz"], w=["zu"])
+    extract(pb[7][:, 0:64], T.zu, 16, T.rowb, True, True, ["zu", "rowb"], ["b7"], np_=16)
+    cp(T.parh[:], T.parb[:], r=["parb"], w=["parh"])
+    ts(T.ip2[:, 0:1], T.ip[:, 0:1], 15, None, A.bitwise_and, r=["ip"], w=["ip20"])
+    ts(T.ip2[:, 1:2], T.ip[:, 0:1], 4, None, A.arith_shift_right, r=["ip"], w=["ip21"])
+    tt(T.parl[:], T.parb[:], T.parh[:], A.subtract, r=["parb", "parh"], w=["parl"])
+    dma("y", "ph", T.part[0:128:16, :], T.parh[:], r=["parh"], w=["par", "q00", "q01", "q10", "q11"])
+    dma("y", "plo", T.part[1:128:16, :], T.parl[:], r=["parl"], w=["parx"])
+    dma("y", "ac", T.acs[:, PC:K], T.ac[:, PC:K], w=["acs"])
+    cp(T.cols[:, 0:2], T.ip2[:, 0:2], r=["ip20", "ip21"], w=["cols"])
+    ts(T.ia2[:], T.ia[:], 4, 7, A.arith_shift_right, A.bitwise_and, r=["ia"], w=["ia2"])
+    op("v", lambda: V.memset(T.zw[:], 0.0), w=["zw"])
+    pcol, gcol, kcol = T.cols[:, 0:1], T.cols[:, 1:2], T.cols[:, 2:3]
+    ts(T.oh[:], T.iv[:], pcol, None, A.is_equal, r=["iv", "cols"], w=["oh"])
+    ts(T.bw[:], T.ia2[:], gcol, None, A.is_equal, r=["ia2", "cols"], w=["bw"])
+    ts(kcol, pcol, 16.0, 512.0, A.add, A.mult, r=["cols"], w=["kcol"])
+    ncol = T.cols[:, 3:4]
+    ts(ncol, pcol, -1.0, None, A.mult, r=["cols"], w=["ncol"])
+    cp(T.zw[:, 0:160:16], T.bw[:, 0:160:16], r=["bw"], w=["zw"])
+    cp(T.moff[:], pb[6][:, 0:64], w=["moff"], x=["b6"])
+    ts(T.uoff[:], pb[7][:, 0:64], 1.0 / 512, None, A.mult, w=["uoff"], x=["b7"])
+    ts(T.ib2[:], T.ib[:], 127, None, A.bitwise_and, r=["ib"], w=["ib2"])
+    cp(T.us[:], pb[7][:, 0:64], w=["us"], x=["b7"])
+    ts(T.iw[:], T.ib2[:], 0.0, None, A.is_equal, r=["ib2"], w=["iw"])
+
+    def xgather(e, h):
+        src = T.oh[:, 0:16].indirect(T.uoff[:, L[h]])
+        if e == "s":
+            act(T.x[:, H[h]], src, F.Copy, r=["oh", "uoff"], w=["x%d" % h])
+        else:
+            cp(T.x[:, H[h]], src, r=["oh", "uoff"], w=["x%d" % h])
+
+    def mtab(t, e, h):
+        ms = T["ms%d" % t]
+        src = T.tab[:, 0:W].indirect(T.moff[:, L[h]])
+        key = "ms%d%d" % (t, h)
+        if e == "s":
+            act(ms[:, H[h]], src, F.Relu, r=TABK + ["moff"], w=[key], bias=DELTA[t])
+        else:
+            ts(ms[:, H[h]], src, DELTA[t], 0.0, A.add, A.max, r=TABK + ["moff"], w=[key])
+        send(dst_of[t], T["ml%d" % t][:, H[h]], ms[:, H[h]], "am%d%d" % (t, h), [key], False)
+
+    xgather("s", 1)
+    mtab(0, "v", 0)
+    mtab(0, "s", 1)
+    cp(T.noff[:], T.ns[:], r=["ns"], w=["noff"])
+    xgather("s", 0)
+    cp(T.eoff[:], T.ev[:], r=["ev", "ev2"], w=["eoff"])
+
+    def send_ac():
+        if far0:
+            cp(T.acu[:, PC:K], T.acs[:, PC:K], r=["acs"], w=["acu"])
+            send(dst_of[0], T.acl[:, PC:K], T.acu[:, PC:K], "aa0", ["acu"], True)
+            send(dst_of[2], T.ac2[:], T.acs[:], "aa2", ["acs", "acsp"], True)
+        else:
+            send(dst_of[0], T.ac0[:, PC:K], T.acs[:, PC:K], "aa0", ["acs"], True)
+            send(dst_of[1], T.ac1[:], T.acs[:], "aa1", ["acs", "acsp"], True)
+        op("g", lambda: g.iota(T.ee[:], [[0, 16], [0, 130]], 0, 0, allow_small_or_imprecise_dtypes=True), w=["ee"])
+
+    def late_constants():
+        act(T.bp[:], T.bw[:], F.Copy, r=["bw"], w=["bp"], scale=32.0)
+        act(T.bm[:], T.bw[:], F.Copy, r=["bw"], w=["bm"], scale=-32.0)
+        act(T.zk[:], T.zw[:], F.Copy, r=["zw", "kcol"], w=["zk"], scale=kcol)
+        act(T.za0[:], T.zw[:], F.Copy, r=["zw"], w=["za0"], scale=float(BIG + BASE))
+        act(T.za1[:], T.zw[:], F.Copy, r=["zw"], w=["za1"], scale=float(BIG + BASE + K))
+        act(T.ze[:], T.zw[:], F.Copy, r=["zw"], w=["ze"], scale=float(BIG))
+        for rg in range(2):
+            c0 = BASE + K * rg
+            mm([(pb[7][:, 64 * rg:64 * rg + 64], T.zw[:, 16 - k:144 - k], T.part[:, c0 + k:c0 + K:16], k == 0, k == 15)
+                for k in range(16)], ["zw"] + PARK, ["b7"])
+        for rg in range(2):
+            act(T["op%d" % rg][:], pb[7][:, 64 * rg:64 * rg + 64], F.Copy, w=["op%d" % rg], x=["b7"])
+
+    def hand_on():
+        for t in range(1, 3):
+            for q in range(N):
+                if q != rank and ac_sender(q, t) == rank:
+                    mine = [s for s in range(3) if src_of[s] == q][0]
+                    send((q - 1 - t) % N, T["ac%d" % t][:], T["ac%d" % mine][:], "aa%d" % t, ["ac%d" % mine, "ac0p"], True)
+
+    def new_e(step):
+        if step == 0:
+            tt(T.me[:], pb[7][:, 0:64], T.ev[:], A.max, r=["ev", "ev2"], w=["me"], x=["b7"])
+        elif step == 1:
+            ts(T.ev[:], T.me[:], BIG - 1, None, A.bitwise_and, r=["me"], w=["ev"])
+        elif step == 2:
+            cp(T.eoff[:], T.ev[:], r=["ev"], w=["eoff"])
+        else:
+            cp(T.fine[:], T.ev[:], r=["ev"], w=["fine"])
+
+    B, Bha = T.bw[:, 16:144], T.bw[:, 0:128]
+    Up, Kp = pb[6][:, 64:128], pb[2][:, 0:64]
+    MK, Y3 = ["mk0", "mk1"], ["y30", "y31"]
+
+    for t in range(RO):
+        last = t == RO - 1
+        rg = t % 2
+        S0 = BASE + K * rg
+        ml, ac, ack = T["ml%d" % t], T["ac%d" % (t % 3)], "ac%d" % (t % 3)
+        act(T.p1[:], T.part[:, 0:W].indirect(T.noff[:, 0:64]), F.Copy, r=PARK + ["noff"], w=["p1"])
+        if not last:
+            for h in range(2):
+                mm([(pb[4 + h][:], T.iw[:, 0:128], T.tab[:, S0 + 512 * h:S0 + 512 * h + 512], True, False)],
+                   ["iw", "t%d%d" % (rg, h)], ["b%d" % (4 + h)])
+        for h in (1, 0):
+            tt(T.y1[:, H[h]], T.tab[:, 0:W].indirect(T.noff[:, L[h]]), T.x[:, H[h]], A.mult,
+               r=TABK + ["noff", "x%d" % h], w=["y1%d" % h])
+            mm([(pb[h][:], B, T.y1[:, H[h]], True, True)], ["bw", "y1%d" % h], ["b%d" % h])
+            if t > 0:
+                new_e(1 - h)
+        extract(Up, T.zw, 16, T.p1, True, True, ["zw", "p1"], ["b6"])
+        if t == 0:
+            send_ac()
+        act(T.r1[:, H[1]], pb[1][:], F.Abs, r=["ncol"], w=["r11"], x=["b1"], bias=ncol)
+        act(T.m1[:, H[1]], T.r1[:, H[1]], F.Relu, r=["r11"], w=["m11"], bias=1.0, scale=-8.0)
+        if t > 0:
+            new_e(2)
+        ts(T.m1[:, H[0]], pb[0][:], pcol, None, A.is_equal, r=["cols"], w=["m10"], x=["b0"])
+        cp(T.n1off[:], Up, w=["n1off"], x=["b6"])
+        for h in (1, 0):
+            mm([(pb[2 + h][:], Bha, T.m1[:, H[h]], True, False)], ["bw", "m1%d" % h], ["b%d" % (2 + h)])
+        if last:
+            extract(pb[4][:, 0:64], T.zk, 16, T.x, True, True, ["zk", "x0", "x1"], ["b4"], block=True)
+        for h in range(2):
+            tt(T.y2[:, H[h]], T.tab[:, 0:W].indirect(T.n1off[:, L[h]]), T.m1[:, H[h]], A.mult,
+               r=TABK + ["n1off", "m1%d" % h], w=["y2%d" % h])
+        if t == 0:
+            late_constants()
+        for h in range(2):
+            act(T.z[:, H[h]], ml[:, 0:K].indirect(T.eoff[:, L[h]]), F.Identity,
+                r=["ml%d0" % t, "ml%d1" % t, "eoff"], w=["z%d" % h], bias=1.0 - DELTA[t])
+        for h in range(2):
+            mm([(pb[2 + h][:], Bha, T.y2[:, H[h]], False, True)], ["bw", "y2%d" % h], ["b%d" % (2 + h)])
+            if not last:
+                mm([(pb[h][:], T.iw[:, 16:144], T.z[:, H[h]], True, False)], ["iw", "z%d" % h], ["b%d" % h])
+        for h in range(2):
+            tt(T.mk[:, H[h]], pb[2 + h][:], T.z[:, H[h]], A.is_equal, r=["z%d" % h], w=["mk%d" % h], x=["b%d" % (2 + h)])
+            if not last:
+                mm([(pb[h][:], T.bm[:, 32:160], T.mk[:, H[h]], False, True)], ["bm", "mk%d" % h], ["b%d" % h])
+                act(T.r1[:, H[h]], pb[h][:], F.Identity, w=["r1%d" % h], x=["b%d" % h], bias=31.0)
+                mm([(pb[4 + h][:], T.bp[:, 32:160], T.mk[:, H[h]], False, True)], ["bp", "mk%d" % h], ["b%d" % (4 + h)])
+        cp(T.up[:], Up, w=["up"], x=["b6"])
+        extract(Kp, T.zk, 32, T.mk, True, True, ["zk"] + MK, ["b2"], block=last)
+        extract(pb[6][:, 0:64], T["za%d" % rg], 32, T.mk, True, False, ["za%d" % rg] + MK, ["b6"])
+        extract(pb[7][:, 0:64], T.ze, 16, T.mk, True, False, ["ze"] + MK, ["b7"])
+        if last:
+            ts(T.ub[:], pb[4][:, 0:64], float(-BIG), None, A.add, w=["ub"], x=["b4"])
+        else:
+            opk = "op%d" % t
+            tt(T.dn[:], T.ns[:], T[opk][:], A.subtract, r=["ns", opk], w=["dn"])
+            for h in range(2):
+                tt(T.tab[:, S0 + 512 * h:S0 + 512 * h + 512], pb[4 + h][:], T.r1[:, H[h]], A.min,
+                   r=["r1%d" % h], w=["t%d%d" % (rg, h)], x=["b%d" % (4 + h)])
+            mtab(t + 1, "s", 0)
+            mtab(t + 1, "s", 1)
+            tt(T.um[:], Kp, T.us[:], A.max, r=["us"], w=["um"], x=["b2"])
+            ts(T.okf[:], Kp, 1.0, None, A.is_ge, w=["okf"], x=["b2"])
+            ts(T.us[:], T.um[:], BIG - 1, None, A.bitwise_and, r=["um"], w=["us"])
+            tt(T.tq[:], T.dn[:], T.okf[:], A.mult, r=["dn", "okf"], w=["tq"])
+            ts(T.uoff[:], T.us[:], 1.0 / 512, None, A.mult, r=["us"], w=["uoff"])
+            xgather("s", 0)
+            pn, pnk = (T.op2, "op2") if t == 0 else (T.pnx, "pnx")
+            tt(pn[:], T.tq[:], T[opk][:], A.add, r=["tq", opk], w=[pnk])
+        if t == 0:
+            ts(T.ee[:, :, 1:129:16], T.ic[:], 0.0, None, A.is_equal, r=["ic"], w=["ee"])
+        if t == 0 and far0_in:
+            cp(T.ac0[:, PC:K], T.acl[:, PC:K], r=["acl"], w=["ac0"])
+            hand_on()
+
+        def move(h):
+            tt(T.y3[:, H[h]], ac[:, 0:K].indirect(T.eoff[:, L[h]]), T.mk[:, H[h]], A.mult,
+               r=[ack, "ac0p", "eoff", "mk%d" % h], w=["y3%d" % h])
+        move(0)
+        if not last:
+            cp(T.pnh[:], pn[:], r=[pnk], w=["pnh"])
+            tt(T.pnl[:], pn[:], T.pnh[:], A.subtract, r=[pnk, "pnh"], w=["pnl"])
+            for h in range(2):
+                it = []
+                for a in range(8):
+                    o = pb[2 + h][:, a:512:8]
+                    it.append((o, T.ee[:, 2 * a + h, 1:129], T.pnh[:], True, False))
+                    it.append((o, T.ee[:, 2 * a + h, 0:128], T.pnl[:], False, True))
+                mm(it, ["ee", "pnh", "pnl"], ["b%d" % (2 + h)])
+                act(T.part[:, S0 + h:S0 + K:2], pb[2 + h][:], F.Copy,
+                    w=["q%d%d" % (rg, h)], x=["b%d" % (2 + h)])
+        move(1)
+        extract(pb[6][:, 0:64], T.zw, 32, T.y3, False, True, ["zw"] + Y3, ["b6"])
+        extract(pb[7][:, 0:64], T.zw, 16, T.y3, False, True, ["zw"] + Y3, ["b7"])
+        if not last:
+            xgather("v", 1)
+        else:
+            tt(T.um[:], Kp, T.ub[:], A.max, r=["ub"], w=["um"], x=["b2"])
+            ts(T.us[:], T.um[:], BIG - 1, None, A.bitwise_and, r=["um"], w=["us"])
+            ts(T.finu[:], T.us[:], 1.0 / 512, None, A.mult, r=["us"], w=["finu"])
+            dma("s", "yu", T.yu[:], T.finu[:], r=["finu"])
+        tt(T.mn[:], pb[6][:, 0:64], T.up[:], A.max, r=["up"], w=["mn"], x=["b6"])
+        if last:
+            new_e(0)
+        ts(T.ns[:], T.mn[:], BIG - 1, None, A.bitwise_and, r=["mn"], w=["ns"])
+        if not last:
+            cp(T.noff[:], T.ns[:], r=["ns"], w=["noff"])
+        else:
+            new_e(1)
+            cp(T.finn[:], T.ns[:], r=["ns"], w=["finn"])
+            new_e(3)
+            dma("y", "yn", T.yn[:], T.finn[:], r=["finn"])
+            dma("s", "yea", T.ye[0:112, :], T.fine[16:128, :], r=["fine"])
+            dma("y", "yeb", T.ye[112:128, :], T.fine[0:16, :], r=["fine"])
+
+    for s, v in cnt.items():
+        if known["g"].get(s, 0) < v:
+            g.wait_ge(T.sem[s], v)

@@ -16,6 +16,10 @@ SCRATCH = {
     "rowf": ("sbuf", [16, K], "float32"),
     "rowb": ("sbuf", [16, K], "bfloat16"),
     "acs": ("sbuf", [128, K], "int32"),
+    "acq": ("sbuf", [128, K], "int32"),
+    "ds": ("sbuf", [128, 64], "float32"),
+    "up2": ("sbuf", [128, 64], "float32"),
+    "tq2": ("sbuf", [128, 64], "float32"),
     "acu": ("sbuf", [128, K], "uint16"),
     "acl": ("sbuf", [128, K], "uint16"),
     "ac0": ("sbuf", [128, K], "int32"),
@@ -68,7 +72,7 @@ SCRATCH = {
     "zm": ("sbuf", [16, 144], "float32"),
     "zu": ("sbuf", [16, 144], "bfloat16"),
     "bw": ("sbuf", [128, 160], "bfloat16"),
-    "bp": ("sbuf", [128, 160], "bfloat16"),
+    "im": ("sbuf", [128, 160], "bfloat16"),
     "bm": ("sbuf", [128, 160], "bfloat16"),
     "iw": ("sbuf", [128, 160], "bfloat16"),
     "zw": ("sbuf", [128, 160], "bfloat16"),
@@ -76,6 +80,8 @@ SCRATCH = {
     "za0": ("sbuf", [128, 160], "bfloat16"),
     "za1": ("sbuf", [128, 160], "bfloat16"),
     "ze": ("sbuf", [128, 160], "bfloat16"),
+    "xw": ("sbuf", [128, 128], "bfloat16"),
+    "xw2": ("sbuf", [128, 128], "bfloat16"),
     "oh": ("sbuf", [128, 16], "bfloat16"),
     "ee": ("sbuf", [128, 16, 130], "bfloat16"),
 }
@@ -242,11 +248,12 @@ def rank_program(g, core, T, topo):
     op("g", lambda: g.iota(T.iv[:], [[1, 16]], 0, 0), w=["iv"])
     op("g", lambda: g.iota(T.ib[:], [[1, 160]], 128, -1), w=["ib"])
     op("g", lambda: g.iota(T.ic[:], [[-1, 16], [-16, 8]], 0, 1), w=["ic"])
-    send(dst_of[0], T.ac0[:, 0:PC], T.acs[:, 0:PC], "aap", ["acsp"], False)
 
     op("v", lambda: V.memset(T.part[:], 0.0), w=PARK)
     ts(T.zm[:], T.iz[:], 0.0, None, A.is_equal, r=["iz"], w=["zm"])
     cp(T.rowf[:], T.rows[:], r=["rows0", "rows1"], w=["rowf"])
+    ts(T.acq[:, 0:PC], T.acs[:, 0:PC], float(K), None, A.add, r=["acsp"], w=["acqp"])
+    send(dst_of[0], T.ac0[:, 0:PC], T.acq[:, 0:PC], "aap", ["acqp"], False)
     extract(pb[6][:, 0:64], T.zm, 16, T.rowf, True, True, ["zm", "rowf"], ["b6"], np_=16)
     act(T.rowb[:], T.rowf[:], F.Copy, r=["rowf"], w=["rowb"])
     ts(T.zu[:], T.iz[:], -128.0, 512.0, A.is_equal, A.mult, r=["iz"], w=["zu"])
@@ -271,7 +278,6 @@ def rank_program(g, core, T, topo):
     cp(T.moff[:], pb[6][:, 0:64], w=["moff"], x=["b6"])
     ts(T.uoff[:], pb[7][:, 0:64], 1.0 / 512, None, A.mult, w=["uoff"], x=["b7"])
     ts(T.ib2[:], T.ib[:], 127, None, A.bitwise_and, r=["ib"], w=["ib2"])
-    cp(T.us[:], pb[7][:, 0:64], w=["us"], x=["b7"])
     ts(T.iw[:], T.ib2[:], 0.0, None, A.is_equal, r=["ib2"], w=["iw"])
 
     def xgather(e, h):
@@ -292,6 +298,7 @@ def rank_program(g, core, T, topo):
         send(dst_of[t], T["ml%d" % t][:, H[h]], ms[:, H[h]], "am%d%d" % (t, h), [key], False)
 
     xgather("s", 1)
+    ts(T.im[:], T.iw[:], -1.0, None, A.mult, r=["iw"], w=["im"])
     mtab(0, "v", 0)
     mtab(0, "s", 1)
     cp(T.noff[:], T.ns[:], r=["ns"], w=["noff"])
@@ -300,21 +307,22 @@ def rank_program(g, core, T, topo):
 
     def send_ac():
         if far0:
-            cp(T.acu[:, PC:K], T.acs[:, PC:K], r=["acs"], w=["acu"])
+            ts(T.acu[:, PC:K], T.acs[:, PC:K], float(K), None, A.add, r=["acs"], w=["acu"])
             send(dst_of[0], T.acl[:, PC:K], T.acu[:, PC:K], "aa0", ["acu"], True)
-            send(dst_of[2], T.ac2[:], T.acs[:], "aa2", ["acs", "acsp"], True)
         else:
-            send(dst_of[0], T.ac0[:, PC:K], T.acs[:, PC:K], "aa0", ["acs"], True)
-            send(dst_of[1], T.ac1[:], T.acs[:], "aa1", ["acs", "acsp"], True)
+            ts(T.acq[:, PC:K], T.acs[:, PC:K], float(K), None, A.add, r=["acs"], w=["acq"])
+            send(dst_of[0], T.ac0[:, PC:K], T.acq[:, PC:K], "aa0", ["acq"], True)
+            send(dst_of[1], T.ac1[:], T.acq[:], "aa1", ["acq", "acqp"], True)
         op("g", lambda: g.iota(T.ee[:], [[0, 16], [0, 130]], 0, 0, allow_small_or_imprecise_dtypes=True), w=["ee"])
 
     def late_constants():
-        act(T.bp[:], T.bw[:], F.Copy, r=["bw"], w=["bp"], scale=32.0)
-        act(T.bm[:], T.bw[:], F.Copy, r=["bw"], w=["bm"], scale=-32.0)
+        act(T.bm[:], T.bw[:], F.Copy, r=["bw"], w=["bm"], scale=-64.0)
+        act(T.xw2[:], T.iw[:, 16:144], F.Copy, r=["iw"], w=["xw2"], scale=2.0)
+        tt(T.xw[:], T.bw[:, 32:160], T.xw2[:], A.subtract, r=["xw2", "bw"], w=["xw"])
         act(T.zk[:], T.zw[:], F.Copy, r=["zw", "kcol"], w=["zk"], scale=kcol)
-        act(T.za0[:], T.zw[:], F.Copy, r=["zw"], w=["za0"], scale=float(BIG + BASE))
-        act(T.za1[:], T.zw[:], F.Copy, r=["zw"], w=["za1"], scale=float(BIG + BASE + K))
-        act(T.ze[:], T.zw[:], F.Copy, r=["zw"], w=["ze"], scale=float(BIG))
+        if far0:
+            ts(T.acq[:, PC:K], T.acs[:, PC:K], float(K), None, A.add, r=["acs"], w=["acq"])
+            send(dst_of[2], T.ac2[:], T.acq[:], "aa2", ["acq", "acqp"], True)
         for rg in range(2):
             c0 = BASE + K * rg
             mm([(pb[7][:, 64 * rg:64 * rg + 64], T.zw[:, 16 - k:144 - k], T.part[:, c0 + k:c0 + K:16], k == 0, k == 15)
@@ -333,7 +341,7 @@ def rank_program(g, core, T, topo):
         if step == 0:
             tt(T.me[:], pb[7][:, 0:64], T.ev[:], A.max, r=["ev", "ev2"], w=["me"], x=["b7"])
         elif step == 1:
-            ts(T.ev[:], T.me[:], BIG - 1, None, A.bitwise_and, r=["me"], w=["ev"])
+            ts(T.ev[:], T.me[:], K - 1, None, A.bitwise_and, r=["me"], w=["ev"])
         elif step == 2:
             cp(T.eoff[:], T.ev[:], r=["ev"], w=["eoff"])
         else:
@@ -356,18 +364,28 @@ def rank_program(g, core, T, topo):
         for h in (1, 0):
             tt(T.y1[:, H[h]], T.tab[:, 0:W].indirect(T.noff[:, L[h]]), T.x[:, H[h]], A.mult,
                r=TABK + ["noff", "x%d" % h], w=["y1%d" % h])
-            mm([(pb[h][:], B, T.y1[:, H[h]], True, True)], ["bw", "y1%d" % h], ["b%d" % h])
+            mm([(pb[2 + h][:], B, T.y1[:, H[h]], True, True)], ["bw", "y1%d" % h], ["b%d" % (2 + h)])
+            if t > 0 and h == 1:
+                tt(T.x[:, H[0]], pb[0][:], T.x[:, H[0]], A.is_lt, r=["x0"], w=["x0"], x=["b0"])
             if t > 0:
                 new_e(1 - h)
-        extract(Up, T.zw, 16, T.p1, True, True, ["zw", "p1"], ["b6"])
+            if h == 0:
+                extract(Up, T.zw, 16, T.p1, True, True, ["zw", "p1"], ["b6"])
+            if not last:
+                mm([(pb[1 - h][:], T.im[:, 0:128], T.tab[:, S0 + 512 * (1 - h):S0 + 512 * (1 - h) + 512], True, False)],
+                   ["im", "t%d%d" % (rg, 1 - h)], ["b%d" % (1 - h)])
         if t == 0:
             send_ac()
-        act(T.r1[:, H[1]], pb[1][:], F.Abs, r=["ncol"], w=["r11"], x=["b1"], bias=ncol)
+        act(T.r1[:, H[1]], pb[3][:], F.Abs, r=["ncol"], w=["r11"], x=["b3"], bias=ncol)
         act(T.m1[:, H[1]], T.r1[:, H[1]], F.Relu, r=["r11"], w=["m11"], bias=1.0, scale=-8.0)
+        opk = "op%d" % t
+        if 0 < t < RO - 1:
+            tt(T.dn[:], T.ns[:], T[opk][:], A.subtract, r=["ns", opk], w=["dn"])
         if t > 0:
             new_e(2)
-        ts(T.m1[:, H[0]], pb[0][:], pcol, None, A.is_equal, r=["cols"], w=["m10"], x=["b0"])
+        ts(T.m1[:, H[0]], pb[2][:], pcol, None, A.is_equal, r=["cols"], w=["m10"], x=["b2"])
         cp(T.n1off[:], Up, w=["n1off"], x=["b6"])
+        cp(T.up[:], Up, w=["up"], x=["b6"])
         for h in (1, 0):
             mm([(pb[2 + h][:], Bha, T.m1[:, H[h]], True, False)], ["bw", "m1%d" % h], ["b%d" % (2 + h)])
         if last:
@@ -375,84 +393,88 @@ def rank_program(g, core, T, topo):
         for h in range(2):
             tt(T.y2[:, H[h]], T.tab[:, 0:W].indirect(T.n1off[:, L[h]]), T.m1[:, H[h]], A.mult,
                r=TABK + ["n1off", "m1%d" % h], w=["y2%d" % h])
+        ts(T.ds[:], Up, -1.0, float(S0 - K), A.mult, A.add, w=["ds"], x=["b6"])
         if t == 0:
             late_constants()
+            tt(T.dn[:], T.ns[:], T[opk][:], A.subtract, r=["ns", opk], w=["dn"])
         for h in range(2):
             act(T.z[:, H[h]], ml[:, 0:K].indirect(T.eoff[:, L[h]]), F.Identity,
                 r=["ml%d0" % t, "ml%d1" % t, "eoff"], w=["z%d" % h], bias=1.0 - DELTA[t])
         for h in range(2):
             mm([(pb[2 + h][:], Bha, T.y2[:, H[h]], False, True)], ["bw", "y2%d" % h], ["b%d" % (2 + h)])
             if not last:
-                mm([(pb[h][:], T.iw[:, 16:144], T.z[:, H[h]], True, False)], ["iw", "z%d" % h], ["b%d" % h])
+                mm([(pb[h][:], T.iw[:, 16:144], T.z[:, H[h]], False, False)], ["iw", "z%d" % h], ["b%d" % h])
         for h in range(2):
             tt(T.mk[:, H[h]], pb[2 + h][:], T.z[:, H[h]], A.is_equal, r=["z%d" % h], w=["mk%d" % h], x=["b%d" % (2 + h)])
             if not last:
                 mm([(pb[h][:], T.bm[:, 32:160], T.mk[:, H[h]], False, True)], ["bm", "mk%d" % h], ["b%d" % h])
-                act(T.r1[:, H[h]], pb[h][:], F.Identity, w=["r1%d" % h], x=["b%d" % h], bias=31.0)
-                mm([(pb[4 + h][:], T.bp[:, 32:160], T.mk[:, H[h]], False, True)], ["bp", "mk%d" % h], ["b%d" % (4 + h)])
-        cp(T.up[:], Up, w=["up"], x=["b6"])
-        extract(Kp, T.zk, 32, T.mk, True, True, ["zk"] + MK, ["b2"], block=last)
-        extract(pb[6][:, 0:64], T["za%d" % rg], 32, T.mk, True, False, ["za%d" % rg] + MK, ["b6"])
-        extract(pb[7][:, 0:64], T.ze, 16, T.mk, True, False, ["ze"] + MK, ["b7"])
+                act(T.r1[:, H[h]], pb[h][:], F.Abs, w=["r1%d" % h], x=["b%d" % h], bias=31.0)
+                mm([(pb[4 + h][:], T.iw[:, 16:144], T.z[:, H[h]], False, False)], ["iw", "z%d" % h], ["b%d" % (4 + h)])
         if last:
+            extract(Kp, T.zk, 32, T.mk, True, True, ["zk"] + MK, ["b2"], block=True)
             ts(T.ub[:], pb[4][:, 0:64], float(-BIG), None, A.add, w=["ub"], x=["b4"])
+            extract(pb[3][:, 0:64], T.zw, 32, T.mk, True, True, ["zw"] + MK, ["b3"])
         else:
-            opk = "op%d" % t
-            tt(T.dn[:], T.ns[:], T[opk][:], A.subtract, r=["ns", opk], w=["dn"])
             for h in range(2):
-                tt(T.tab[:, S0 + 512 * h:S0 + 512 * h + 512], pb[4 + h][:], T.r1[:, H[h]], A.min,
-                   r=["r1%d" % h], w=["t%d%d" % (rg, h)], x=["b%d" % (4 + h)])
-            mtab(t + 1, "s", 0)
-            mtab(t + 1, "s", 1)
-            tt(T.um[:], Kp, T.us[:], A.max, r=["us"], w=["um"], x=["b2"])
-            ts(T.okf[:], Kp, 1.0, None, A.is_ge, w=["okf"], x=["b2"])
-            ts(T.us[:], T.um[:], BIG - 1, None, A.bitwise_and, r=["um"], w=["us"])
-            tt(T.tq[:], T.dn[:], T.okf[:], A.mult, r=["dn", "okf"], w=["tq"])
-            ts(T.uoff[:], T.us[:], 1.0 / 512, None, A.mult, r=["us"], w=["uoff"])
-            xgather("s", 0)
-            pn, pnk = (T.op2, "op2") if t == 0 else (T.pnx, "pnx")
-            tt(pn[:], T.tq[:], T[opk][:], A.add, r=["tq", opk], w=[pnk])
+                if h == 1:
+                    extract(Kp, T.zw, 32, T.mk, True, True, ["zw"] + MK, ["b2"])
+                mm([(pb[4 + h][:], T.im[:, 0:128], T.r1[:, H[h]], False, True)], ["im", "r1%d" % h], ["b%d" % (4 + h)])
+                act(T.tab[:, S0 + 512 * h:S0 + 512 * h + 512], pb[4 + h][:], F.Identity,
+                    w=["t%d%d" % (rg, h)], x=["b%d" % (4 + h)], scale=0.5, bias=15.5)
         if t == 0:
             ts(T.ee[:, :, 1:129:16], T.ic[:], 0.0, None, A.is_equal, r=["ic"], w=["ee"])
         if t == 0 and far0_in:
             cp(T.ac0[:, PC:K], T.acl[:, PC:K], r=["acl"], w=["ac0"])
-            hand_on()
 
         def move(h):
             tt(T.y3[:, H[h]], ac[:, 0:K].indirect(T.eoff[:, L[h]]), T.mk[:, H[h]], A.mult,
                r=[ack, "ac0p", "eoff", "mk%d" % h], w=["y3%d" % h])
         move(0)
         if not last:
+            mtab(t + 1, "s", 0)
+            mtab(t + 1, "s", 1)
+            if t == 0 and far0_in:
+                hand_on()
+            move(1)
+            pn, pnk = (T.op2, "op2") if t == 0 else (T.pnx, "pnx")
+
+            def xsum(h):
+                mm([(pb[h][:], T.xw[:], T.mk[:, H[h]], True, True)], ["xw", "mk%d" % h], ["b%d" % h])
+            xsum(1)
+            extract(pb[6][:, 0:64], T.zw, 32, T.y3, True, True, ["zw"] + Y3, ["b6"])
+            tt(T.tq[:], Kp, T.dn[:], A.mult, r=["dn"], w=["tq"], x=["b2"])
+            tt(T.tq2[:], Kp, T.ds[:], A.mult, r=["ds"], w=["tq2"], x=["b2"])
+            tt(pn[:], T.tq[:], T[opk][:], A.add, r=["tq", opk], w=[pnk])
             cp(T.pnh[:], pn[:], r=[pnk], w=["pnh"])
+            tt(T.up2[:], T.tq2[:], T.up[:], A.add, r=["tq2", "up"], w=["up2"])
             tt(T.pnl[:], pn[:], T.pnh[:], A.subtract, r=[pnk, "pnh"], w=["pnl"])
-            for h in range(2):
+            tt(T.ns[:], pb[6][:, 0:64], T.up2[:], A.add, r=["up2"], w=["ns"], x=["b6"])
+            for h in (1, 0):
                 it = []
                 for a in range(8):
                     o = pb[2 + h][:, a:512:8]
                     it.append((o, T.ee[:, 2 * a + h, 1:129], T.pnh[:], True, False))
                     it.append((o, T.ee[:, 2 * a + h, 0:128], T.pnl[:], False, True))
                 mm(it, ["ee", "pnh", "pnl"], ["b%d" % (2 + h)])
-                act(T.part[:, S0 + h:S0 + K:2], pb[2 + h][:], F.Copy,
-                    w=["q%d%d" % (rg, h)], x=["b%d" % (2 + h)])
-        move(1)
-        extract(pb[6][:, 0:64], T.zw, 32, T.y3, False, True, ["zw"] + Y3, ["b6"])
-        extract(pb[7][:, 0:64], T.zw, 16, T.y3, False, True, ["zw"] + Y3, ["b7"])
-        if not last:
-            xgather("v", 1)
+            xsum(0)
+            extract(pb[7][:, 0:64], T.zw, 16, T.y3, True, True, ["zw"] + Y3, ["b7"])
+            tt(T.x[:, H[1]], pb[1][:], T.x[:, H[1]], A.is_lt, r=["x1"], w=["x1"], x=["b1"])
+            cp(T.noff[:], T.ns[:], r=["ns"], w=["noff"])
+            cp(T.part[:, S0 + 1:S0 + K:2], pb[3][:], w=["q%d1" % rg], x=["b3"])
+            act(T.part[:, S0:S0 + K:2], pb[2][:], F.Copy, w=["q%d0" % rg], x=["b2"])
         else:
+            move(1)
+            extract(pb[7][:, 0:64], T.zw, 16, T.y3, True, True, ["zw"] + Y3, ["b7"])
+            extract(pb[6][:, 0:64], T.zw, 32, T.y3, True, True, ["zw"] + Y3, ["b6"])
             tt(T.um[:], Kp, T.ub[:], A.max, r=["ub"], w=["um"], x=["b2"])
+            tt(T.tq2[:], pb[3][:, 0:64], T.ds[:], A.mult, r=["ds"], w=["tq2"], x=["b3"])
             ts(T.us[:], T.um[:], BIG - 1, None, A.bitwise_and, r=["um"], w=["us"])
+            tt(T.up2[:], T.tq2[:], T.up[:], A.add, r=["tq2", "up"], w=["up2"])
             ts(T.finu[:], T.us[:], 1.0 / 512, None, A.mult, r=["us"], w=["finu"])
             dma("s", "yu", T.yu[:], T.finu[:], r=["finu"])
-        tt(T.mn[:], pb[6][:, 0:64], T.up[:], A.max, r=["up"], w=["mn"], x=["b6"])
-        if last:
             new_e(0)
-        ts(T.ns[:], T.mn[:], BIG - 1, None, A.bitwise_and, r=["mn"], w=["ns"])
-        if not last:
-            cp(T.noff[:], T.ns[:], r=["ns"], w=["noff"])
-        else:
             new_e(1)
-            cp(T.finn[:], T.ns[:], r=["ns"], w=["finn"])
+            tt(T.finn[:], pb[6][:, 0:64], T.up2[:], A.add, r=["up2"], w=["finn"], x=["b6"])
             new_e(3)
             dma("y", "yn", T.yn[:], T.finn[:], r=["finn"])
             dma("s", "yea", T.ye[0:112, :], T.fine[16:128, :], r=["fine"])

@@ -3,153 +3,148 @@ from concourse.mybir import AluOpType, ActivationFunctionType
 A = AluOpType
 F = ActivationFunctionType
 BASE, K, W, RO = 2560, 1024, 4608, 4
-DELTA = [0.75, 0.5, 0.25, 0.125]
-BIG = 8192
+HOLE = [0.25, 0.5, 0.75, 0.875]
+NCH = 4
+CW = W // NCH
+PF = 3072
+AC_EARLY = [1]
+AC_NEAR = [0]
+HELP = [0]
+RADIX = 96
+UPC = -64.0 * (RADIX + 1)
+PUSH = ["sv", "ss", "ss", "ss"]
+PLAN = dict(cyc=0.00087, pe=0.00044, gather=1.4, hop=0.2, issue=0.3, load0=1.6, load=0.0025, push=2.5, link=1.2, ac=3.0, rounds=6)
 
 SCRATCH = {
+    "raw": ("sbuf", [128, W], "bfloat16"),
     "tab": ("sbuf", [128, W], "bfloat16"),
     "part": ("sbuf", [128, W], "bfloat16"),
     "parb": ("sbuf", [128, 288], "int32"),
-    "parh": ("sbuf", [128, 288], "bfloat16"),
-    "parl": ("sbuf", [128, 288], "bfloat16"),
+    "nn": ("sbuf", [128, 288], "float32"),
+    "du": ("sbuf", [128, 288], "float32"),
     "rows": ("sbuf", [16, K], "int32"),
     "rowf": ("sbuf", [16, K], "float32"),
     "rowb": ("sbuf", [16, K], "bfloat16"),
     "acs": ("sbuf", [128, K], "int32"),
-    "acq": ("sbuf", [128, K], "int32"),
-    "ds": ("sbuf", [128, 64], "float32"),
-    "up2": ("sbuf", [128, 64], "float32"),
-    "tq2": ("sbuf", [128, 64], "float32"),
-    "acu": ("sbuf", [128, K], "uint16"),
-    "acl": ("sbuf", [128, K], "uint16"),
-    "ac0": ("sbuf", [128, K], "int32"),
-    "ac1": ("sbuf", [128, K], "int32"),
-    "ac2": ("sbuf", [128, K], "int32"),
-    "x": ("sbuf", [128, K], "bfloat16"),
-    "y1": ("sbuf", [128, K], "bfloat16"),
-    "p1": ("sbuf", [128, K], "bfloat16"),
-    "m1": ("sbuf", [128, K], "bfloat16"),
-    "y2": ("sbuf", [128, K], "bfloat16"),
-    "z": ("sbuf", [128, K], "bfloat16"),
-    "mk": ("sbuf", [128, K], "bfloat16"),
-    "r1": ("sbuf", [128, K], "bfloat16"),
     "y3": ("sbuf", [128, K], "float16"),
-    "moff": ("sbuf", [128, 64], "uint16"),
-    "n1off": ("sbuf", [128, 64], "uint16"),
-    "uoff": ("sbuf", [128, 64], "uint16"),
-    "us": ("sbuf", [128, 64], "int32"),
-    "um": ("sbuf", [128, 64], "int32"),
-    "ub": ("sbuf", [128, 64], "int32"),
-    "up": ("sbuf", [128, 64], "int32"),
-    "op0": ("sbuf", [128, 64], "float32"),
-    "op1": ("sbuf", [128, 64], "float32"),
-    "op2": ("sbuf", [128, 64], "float32"),
-    "pnx": ("sbuf", [128, 64], "float32"),
-    "dn": ("sbuf", [128, 64], "float32"),
-    "okf": ("sbuf", [128, 64], "float32"),
-    "tq": ("sbuf", [128, 64], "float32"),
-    "pnh": ("sbuf", [128, 64], "bfloat16"),
-    "pnl": ("sbuf", [128, 64], "bfloat16"),
-    "mn": ("sbuf", [128, 64], "int32"),
-    "me": ("sbuf", [128, 64], "int32"),
     "ns": ("sbuf", [128, 64], "int32"),
     "ev": ("sbuf", [128, 64], "int32"),
-    "noff": ("sbuf", [128, 64], "uint16"),
-    "eoff": ("sbuf", [128, 64], "uint16"),
-    "finn": ("sbuf", [128, 64], "float32"),
-    "fine": ("sbuf", [128, 64], "float32"),
-    "finu": ("sbuf", [128, 64], "float32"),
+    "um": ("sbuf", [128, 64], "int32"),
+    "us": ("sbuf", [128, 64], "int32"),
+    "te": ("sbuf", [128, 64], "float16"),
     "ip": ("sbuf", [128, 8], "int32"),
     "ip2": ("sbuf", [128, 8], "int32"),
-    "cols": ("sbuf", [128, 8], "float32"),
-    "ia": ("sbuf", [128, 160], "int32"),
-    "ib": ("sbuf", [128, 160], "int32"),
-    "ia2": ("sbuf", [128, 160], "int32"),
-    "ib2": ("sbuf", [128, 160], "int32"),
-    "ic": ("sbuf", [128, 16, 8], "int32"),
-    "iv": ("sbuf", [128, 16], "int32"),
-    "iz": ("sbuf", [16, 144], "int32"),
+    "cols": ("sbuf", [128, 16], "float32"),
+    "ia": ("sbuf", [128, 256], "int32"),
+    "ib": ("sbuf", [128, 128], "int32"),
+    "onef": ("sbuf", [16, 144], "float32"),
     "zm": ("sbuf", [16, 144], "float32"),
-    "zu": ("sbuf", [16, 144], "bfloat16"),
-    "bw": ("sbuf", [128, 160], "bfloat16"),
-    "im": ("sbuf", [128, 160], "bfloat16"),
-    "bm": ("sbuf", [128, 160], "bfloat16"),
-    "iw": ("sbuf", [128, 160], "bfloat16"),
-    "zw": ("sbuf", [128, 160], "bfloat16"),
-    "zk": ("sbuf", [128, 160], "bfloat16"),
-    "za0": ("sbuf", [128, 160], "bfloat16"),
-    "za1": ("sbuf", [128, 160], "bfloat16"),
-    "ze": ("sbuf", [128, 160], "bfloat16"),
-    "xw": ("sbuf", [128, 128], "bfloat16"),
-    "xw2": ("sbuf", [128, 128], "bfloat16"),
-    "oh": ("sbuf", [128, 16], "bfloat16"),
-    "ee": ("sbuf", [128, 16, 130], "bfloat16"),
+    "zb": ("sbuf", [16, 128], "bfloat16"),
+    "iwf": ("sbuf", [128, 256], "float32"),
 }
+for _n in ["x", "y1", "p1", "xx", "y2", "z", "mk", "aa"]:
+    SCRATCH[_n] = ("sbuf", [128, K], "bfloat16")
+for _n in ["moff", "noff", "n1off", "eoff"]:
+    SCRATCH[_n] = ("sbuf", [128, 64], "uint16")
+for _n in ["dsn", "tq", "td", "eh", "ub", "finn", "fine", "finu"]:
+    SCRATCH[_n] = ("sbuf", [128, 64], "float32")
+for _n in ["one", "bw", "iw", "zw", "zp", "zn", "zk", "zr"]:
+    SCRATCH[_n] = ("sbuf", [128, 256], "bfloat16")
+for _n in ["bm", "bp", "bx", "xw", "xw2", "wo", "ws", "wf"]:
+    SCRATCH[_n] = ("sbuf", [128, 128], "bfloat16")
+for _t in range(4):
+    SCRATCH["dg%d" % _t] = ("sbuf", [128, 288], "bfloat16")
+for _t in range(3):
+    SCRATCH["ac%d" % _t] = ("sbuf", [128, K], "int32")
 for _t in range(RO):
     SCRATCH["ms%d" % _t] = ("sbuf", [128, K], "bfloat16")
     SCRATCH["ml%d" % _t] = ("sbuf", [128, K], "bfloat16")
 for _b in range(8):
     SCRATCH["pb%d" % _b] = ("psum", [128, 512], "float32")
 
-PC = 128
-DMAS = ["idm", "mnt", "u0", "ac", "acp", "par", "ns0", "e0a", "e0b", "ph", "plo", "yn", "yea", "yeb", "yu"]
-SEMAPHORES = (["cv", "cs", "cp", "cg", "ls", "aa0", "aa1", "aa2", "aap"] + ["d_" + n for n in DMAS]
+DMAS = (["mnt", "u0", "ac0", "ac1", "par", "ns0", "e0", "yn", "ye", "yu"] + ["idm%d" % c for c in range(NCH)]
+        + ["dg%d" % c for c in range(4)])
+SEMAPHORES = (["cv", "cs", "cp", "cg", "ls", "aa00", "aa01", "aa10", "aa11", "aa20", "ah"] + ["d_" + n for n in DMAS]
               + ["am%d%d" % (t, h) for t in range(RO) for h in range(2)])
+
+
+def hazards(calls):
+    lastw, readers, prev, before = {}, {}, {}, []
+    for i, c in enumerate(calls):
+        d = set(c["after"])
+        for k in c["r"] + c["w"] + c["x"]:
+            if k in lastw:
+                d.add(lastw[k])
+        for k in c["w"]:
+            d.update(readers.get(k, []))
+        for k in c["x"]:
+            d.update(j for j in readers.get(k, []) if calls[j]["e"] != c["e"])
+        if c["chain"]:
+            if c["chain"] in prev:
+                d.add(prev[c["chain"]])
+            prev[c["chain"]] = i
+        for k in c["r"] + c["x"]:
+            readers.setdefault(k, []).append(i)
+        for k in c["w"]:
+            lastw[k] = i
+            readers[k] = []
+        before.append(sorted(d))
+    return before
+
+
+def issue_order(calls):
+    n = len(calls)
+    before = hazards(calls)
+    after = [[] for _ in calls]
+    for i in range(n):
+        for j in before[i]:
+            after[j].append(i)
+
+    def gap(j, i):
+        if calls[j]["chain"] and calls[j]["chain"] == calls[i]["chain"]:
+            return calls[j]["busy"]
+        hop = 0.0 if calls[j]["e"] == calls[i]["e"] == "p" else PLAN["hop"]
+        return calls[j]["busy"] + calls[j]["late"] + hop
+
+    def place(order, back):
+        taken, at = {}, [0.0] * n
+        for i in order:
+            busy = calls[i]["busy"]
+            if back:
+                s = max([calls[i]["late"]] + [at[k] + calls[k]["busy"] + gap(i, k) - busy for k in after[i]])
+            else:
+                s = max([0.0] + [at[j] + gap(j, i) for j in before[i]])
+            line = taken.setdefault(calls[i]["e"], [])
+            for a, b in line:
+                if s + busy <= a:
+                    break
+                s = max(s, b)
+            line.append((s, s + busy))
+            line.sort()
+            at[i] = s
+        return at
+
+    way = [0.0] * n
+    for j in reversed(range(n)):
+        way[j] = max([calls[j]["busy"] + calls[j]["late"]] + [gap(j, i) + way[i] for i in after[j]])
+    at = place(sorted(range(n), key=lambda i: (-way[i], i)), False)
+    best = None
+    for _ in range(PLAN["rounds"]):
+        end = max(at[i] + calls[i]["busy"] + calls[i]["late"] for i in range(n))
+        if best is None or end < best[0]:
+            best = (end, at)
+        rev = place(sorted(range(n), key=lambda i: (-at[i] - calls[i]["busy"], -i)), True)
+        at = place(sorted(range(n), key=lambda i: (-rev[i] - calls[i]["busy"], i)), False)
+    PLAN["end"] = best[0]
+    return sorted(range(n), key=lambda i: (best[1][i], i))
 
 
 def rank_program(g, core, T, topo):
     rank = T.rank_of(core)
-    if rank is None:
-        return
     cores = list(T.cores)
     N = len(cores)
-    Q = {"v": g.vector, "s": g.scalar, "p": g.tensor, "g": g, "y": g.sync}
-    CN = {"v": "cv", "s": "cs", "p": "cp", "g": "cg"}
-    cnt = {}
-    known = {e: {} for e in Q}
-    lastw, readers = {}, {}
-
-    def need(e, tok):
-        sem, val, clock, _ = tok
-        if known[e].get(sem, 0) < val:
-            Q[e].wait_ge(T.sem[sem], val)
-            known[e][sem] = val
-        for s, v in clock.items():
-            if known[e].get(s, 0) < v:
-                known[e][s] = v
-
-    def deps(e, r, w, x):
-        toks = []
-        for k in list(r) + list(w) + list(x):
-            if k in lastw and not (e == "p" and lastw[k][3] == "p"):
-                toks.append(lastw[k])
-        for k in w:
-            toks += [tok for tok in readers.get(k, []) if not (e == "p" and tok[3] == "p")]
-        for k in x:
-            toks += [tok for tok in readers.get(k, []) if tok[3] != e]
-        for tok in sorted(toks, key=lambda tk: -tk[1]):
-            need(e, tok)
-
-    def note(tok, r, w, x):
-        for k in list(r) + list(x):
-            readers.setdefault(k, []).append(tok)
-        for k in w:
-            lastw[k] = tok
-            readers[k] = []
-
-    def op(e, fn, r=(), w=(), x=()):
-        deps(e, r, w, x)
-        ins = fn()
-        c = CN[e]
-        cnt[c] = cnt.get(c, 0) + 1
-        ins.then_inc(T.sem[c], 1)
-        note((c, cnt[c], dict(known[e]), e), r, w, x)
-
-    def dma(e, name, out, in_, r=(), w=()):
-        deps(e, r, w, ())
-        Q[e].dma_start(out, in_).then_inc(T.sem["d_" + name], 16)
-        cnt["d_" + name] = 16
-        note(("d_" + name, 16, dict(known[e]), "dma"), r, w, ())
+    H = [slice(0, 512), slice(512, 1024)]
+    L = [slice(0, 32), slice(32, 64)]
 
     def bits(engs):
         return sum(1 << i for i in engs)
@@ -157,329 +152,367 @@ def rank_program(g, core, T, topo):
     def same_chip(a, b):
         return cores[b] in topo.cores_of(cores[a])
 
-    def lanes(src, dst, spare):
-        full = topo.engines(cores[src], cores[dst])
-        if spare and same_chip(src, dst):
-            far = [d for d in range(N) if not same_chip(src, d)][0]
-            off = topo.engines(cores[src], cores[far])
-            return [i for i in full if i not in off]
-        return full
+    def helper(q):
+        return [c for c in topo.cores_of(cores[q]) if c not in cores and topo.die(c) != topo.die(cores[q])][0]
 
-    def send(dst, out, in_, sem, r, spare):
-        deps("g", r, (), ())
-        rid, pid = topo.addr(cores[dst], core)
-        en = lanes(rank, dst, spare)
-        g.remote_dma(out, in_, T.sem[sem], T.sem.ls, pid, rid, bits(en))
-        cnt["ls"] = cnt.get("ls", 0) + len(en)
+    def spare(q):
+        far = [d for d in range(N) if not same_chip(q, d)][0]
+        return [i for i in topo.engines(cores[q], helper(q)) if i not in topo.engines(cores[q], cores[far])]
 
-    def arrives(key, sem, src, spare):
-        n = len(lanes(src, rank, spare))
-        cnt[sem] = n
-        lastw[key] = (sem, n, {}, "rem")
+    def first_far(q):
+        return [s for s in range(3) if not same_chip(q, (q - 1 - s) % N)][0]
 
-    def mm(items, r, w):
+    if rank is None:
+        for q in range(N):
+            if helper(q) == core and first_far(q) in HELP:
+                s = first_far(q)
+                d = cores[(q - 1 - s) % N]
+                g.wait_ge(T.sem.ah, len(spare(q)))
+                rid, pid = topo.addr(d, core)
+                en = topo.engines(core, d)
+                g.remote_dma(T["ac%d" % s][:, H[1]], T.acs[:, H[1]], T.sem["aa%d1" % s], T.sem.ls, pid, rid, bits(en))
+                g.wait_ge(T.sem.ls, len(en))
+        return
+
+    calls = []
+
+    def call(e, fn, sem, busy, r=(), w=(), x=(), late=0.0, chain=None, after=()):
+        calls.append(dict(e=e, fn=fn, sem=sem, busy=busy, late=late, r=list(r), w=list(w), x=list(x), chain=chain, after=list(after)))
+        return len(calls) - 1
+
+    def op(e, fn, n, r=(), w=(), x=()):
+        call(e, fn, "c" + e, n * PLAN["pe"] if e == "p" else max(n, 64) * PLAN["cyc"], r, w, x, chain="g" if e == "g" else None)
+
+    def dma(e, name, out, in_, kib, r=(), w=()):
+        q = {"s": g.scalar, "y": g.sync}[e]
+        call(e, lambda: q.dma_start(out, in_), "d_" + name, 0.05, r, w, chain="dma" + e)
+        call("dma", None, None, kib * PLAN["load"], (), w, late=PLAN["load0"], chain="dma", after=[len(calls) - 1])
+
+    def lanes(src, dst, sp):
+        return spare(src) if sp and same_chip(src, dst) else topo.engines(cores[src], cores[dst])
+
+    def write(to, en, out, in_, sem, r):
+        rid, pid = topo.addr(to, core)
+        call("g", lambda: g.remote_dma(out, in_, T.sem[sem], T.sem.ls, pid, rid, bits(en)), ("ls", len(en)), PLAN["issue"], r, chain="g")
+
+    def send(dst, out, in_, sem, r, sp):
+        write(cores[dst], lanes(rank, dst, sp), out, in_, sem, r)
+
+    def arrives(key, sem, src, sp, late, busy=0.001):
+        call("-", None, (sem, len(lanes(src, rank, sp))), busy, w=[key], late=late, after=[len(calls) - 1])
+
+    def mm(items, n, r, w):
         def fn():
             ins = None
             for (o, l, rh, st, sp) in items:
                 ins = g.tensor.matmul(o, l, rh, st, sp)
             return ins
-        op("p", fn, r=r, w=w)
+        op("p", fn, n, r=r, w=w)
 
     def extract(out, wt, off, src, first, last, r, w, block=False, np_=128):
         it = []
         for k in range(16):
             rh = src[0:np_, 64 * k:64 * k + 64] if block else src[0:np_, k:K:16]
             it.append((out, wt[0:np_, off - k:off - k + 128], rh, first and k == 0, last and k == 15))
-        mm(it, r, w)
+        mm(it, K if np_ == 128 else 4 * K, r, w)
 
     V, S = g.vector, g.scalar
     pb = [T["pb%d" % b] for b in range(8)]
-    H = [slice(0, 512), slice(512, 1024)]
-    L = [slice(0, 32), slice(32, 64)]
-    TABK = ["tab", "t00", "t01", "t10", "t11"]
-    PARK = ["par", "parx", "q00", "q01", "q10", "q11"]
+    TC = ["tc%d" % c for c in range(NCH)]
+    RAWK = ["raw%d" % c for c in range(NCH)]
+    TABK = TC + ["t00", "t01", "t10", "t11"]
+    PD = ["pd%d" % c for c in range(4)]
+    PARK = PD + ["q00", "q01", "q10", "q11"]
     src_of = [(rank + 1 + t % 3) % N for t in range(RO)]
     dst_of = [(rank - 1 - t % 3) % N for t in range(RO)]
     far0 = not same_chip(rank, dst_of[0])
-    far0_in = not same_chip(rank, src_of[0])
+    GA = int(64 + 512 * PLAN["gather"])
 
-    def ts(out, in0, s1, s2, o0, o1=None, r=(), w=(), x=()):
+    def ts(out, in0, s1, s2, o0, o1=None, n=64, r=(), w=(), x=()):
         if o1 is None:
-            op("v", lambda: V.tensor_scalar(out, in0, s1, None, o0), r, w, x)
+            op("v", lambda: V.tensor_scalar(out, in0, s1, None, o0), n, r, w, x)
         else:
-            op("v", lambda: V.tensor_scalar(out, in0, s1, s2, o0, o1), r, w, x)
+            op("v", lambda: V.tensor_scalar(out, in0, s1, s2, o0, o1), n, r, w, x)
 
-    def tt(out, in0, in1, o, r=(), w=(), x=()):
-        op("v", lambda: V.tensor_tensor(out, in0, in1, o), r, w, x)
+    def tt(out, in0, in1, o, n=64, r=(), w=(), x=()):
+        op("v", lambda: V.tensor_tensor(out, in0, in1, o), n, r, w, x)
 
-    def cp(out, in_, r=(), w=(), x=()):
-        op("v", lambda: V.tensor_copy(out, in_), r, w, x)
+    def cp(out, in_, n=64, r=(), w=(), x=()):
+        op("v", lambda: V.tensor_copy(out, in_), n, r, w, x)
 
-    def act(out, in_, f, r=(), w=(), x=(), **kw):
-        op("s", lambda: S.activation(out, in_, f, **kw), r, w, x)
+    def fill(ap, c, n, w):
+        op("v", lambda: V.memset(ap, c), n, w=w)
+
+    def act(out, in_, f, n=64, r=(), w=(), x=(), **kw):
+        op("s", lambda: S.activation(out, in_, f, **kw), n, r, w, x)
+
+    def iota(out, pattern, base, cm, n, w, small=False):
+        op("g", lambda: g.iota(out, pattern, base, cm, allow_small_or_imprecise_dtypes=small), 150 + 2 * n, w=w)
+
+    def where(out, in_, pattern, base, cm, n, r, w):
+        op("g", lambda: g.affine_select(out, in_, pattern, A.is_equal, 0.0, base, cm), 200 + 2 * n, r=r, w=w)
 
     def ac_sender(q, t):
         d = (q - 1 - t) % N
         if same_chip(q, d):
             return q
-        first = [(q - 1 - s) % N for s in range(3) if not same_chip(q, (q - 1 - s) % N)][0]
-        return q if first == d else first
+        return q if first_far(q) == t else (q - 1 - first_far(q)) % N
 
-    for t in range(RO):
-        for h in range(2):
-            arrives("ml%d%d" % (t, h), "am%d%d" % (t, h), src_of[t], False)
-    for t in range(3):
-        arrives("acl" if (t == 0 and far0_in) else "ac%d" % t, "aa%d" % t, ac_sender(src_of[t], t), True)
+    ACK = [["ac%d%d" % (t, h) for h in range(2 if t == 0 or first_far(src_of[t]) == t else 1)] for t in range(3)]
 
-    arrives("ac0p", "aap", src_of[0], False)
+    def ac_arrives(t, late):
+        for k in ACK[t]:
+            arrives(k, "aa" + k[2:], ac_sender(src_of[t], t), True, late)
 
-    dma("s", "mnt", T.rows[0:8, :], T.mnt[:], w=["rows0"])
-    dma("y", "u0", T.rows[8:16, :], T.u0[:], w=["rows1"])
-    dma("s", "par", T.parb[:], T.par[:], w=["parb"])
-    dma("y", "acp", T.acs[:, 0:PC], T.ac[:, 0:PC], w=["acsp"])
-    dma("y", "idm", T.tab[:], T.idm[:], w=TABK)
-    dma("s", "ns0", T.ns[:], T.ns0[:], w=["ns"])
-    dma("s", "e0a", T.ev[16:128, :], T.e0[0:112, :], w=["ev"])
-    dma("s", "e0b", T.ev[0:16, :], T.e0[112:128, :], w=["ev2"])
+    def lift(e, c):
+        sl = slice(CW * c, CW * c + CW)
+        if e == "s":
+            act(T.tab[:, sl], T.raw[:, sl], F.Identity, CW, r=[RAWK[c]], w=[TC[c]], bias=1.0)
+        else:
+            ts(T.tab[:, sl], T.raw[:, sl], 1.0, None, A.add, n=CW // 2, r=[RAWK[c]], w=[TC[c]])
 
-    op("g", lambda: g.iota(T.iz[:], [[1, 144]], -16, -16), w=["iz"])
-    op("g", lambda: g.iota(T.ip[:, 0:1], [[1, 1]], 0, 1), w=["ip"])
-    op("g", lambda: g.iota(T.ia[:], [[1, 160]], 112, 0), w=["ia"])
-    op("g", lambda: g.iota(T.iv[:], [[1, 16]], 0, 0), w=["iv"])
-    op("g", lambda: g.iota(T.ib[:], [[1, 160]], 128, -1), w=["ib"])
-    op("g", lambda: g.iota(T.ic[:], [[-1, 16], [-16, 8]], 0, 1), w=["ic"])
+    def load_ac(h):
+        dma("y", "ac%d" % h, T.acs[:, H[h]], T.ac[:, H[h]], 256, w=["acs%d" % h])
 
-    op("v", lambda: V.memset(T.part[:], 0.0), w=PARK)
-    ts(T.zm[:], T.iz[:], 0.0, None, A.is_equal, r=["iz"], w=["zm"])
-    cp(T.rowf[:], T.rows[:], r=["rows0", "rows1"], w=["rowf"])
-    ts(T.acq[:, 0:PC], T.acs[:, 0:PC], float(K), None, A.add, r=["acsp"], w=["acqp"])
-    send(dst_of[0], T.ac0[:, 0:PC], T.acq[:, 0:PC], "aap", ["acqp"], False)
-    extract(pb[6][:, 0:64], T.zm, 16, T.rowf, True, True, ["zm", "rowf"], ["b6"], np_=16)
-    act(T.rowb[:], T.rowf[:], F.Copy, r=["rowf"], w=["rowb"])
-    ts(T.zu[:], T.iz[:], -128.0, 512.0, A.is_equal, A.mult, r=["iz"], w=["zu"])
-    extract(pb[7][:, 0:64], T.zu, 16, T.rowb, True, True, ["zu", "rowb"], ["b7"], np_=16)
-    cp(T.parh[:], T.parb[:], r=["parb"], w=["parh"])
+    def ac_abroad(h, r=()):
+        ff = first_far(rank)
+        if h == 1 and ff in HELP:
+            write(helper(rank), spare(rank), T.acs[:, H[1]], T.acs[:, H[1]], "ah", ["acs1"] + list(r))
+        else:
+            send(dst_of[ff], T["ac%d" % ff][:, H[h]], T.acs[:, H[h]], "aa%d%d" % (ff, h), ["acs%d" % h] + list(r), True)
+
+    def hand_on(t):
+        for q in range(N):
+            if q != rank and ac_sender(q, t) == rank:
+                mine = src_of.index(q)
+                send((q - 1 - t) % N, T["ac%d" % t][:], T["ac%d" % mine][:], "aa%d0" % t, ACK[mine], True)
+        if far0 and t == 1:
+            send(dst_of[2], T.ac2[:], T.acs[:], "aa20", ["acs0", "acs1"], True)
+
+    def mtab(t, h):
+        ms = T["ms%d" % t]
+        win, keys, sh = (T.raw, RAWK, 1.0) if t == 0 else (T.tab, TABK, 0.0)
+        src = win[:, 0:W].indirect(T.moff[:, L[h]])
+        key = "ms%d%d" % (t, h)
+        if PUSH[t][h] == "s":
+            act(ms[:, H[h]], src, F.Relu, GA, r=keys + ["moff"], w=[key], bias=sh - HOLE[t])
+        else:
+            ts(ms[:, H[h]], src, sh - HOLE[t], 0.0, A.add, A.max, n=GA, r=keys + ["moff"], w=[key])
+        send(dst_of[t], T["ml%d" % t][:, H[h]], ms[:, H[h]], "am%d%d" % (t, h), [key], False)
+        arrives("ml%d%d" % (t, h), "am%d%d" % (t, h), src_of[t], False, PLAN["push"], PLAN["link"])
+
+    early = AC_EARLY if far0 else AC_NEAR
+    dma("s", "mnt", T.rows[0:8, :], T.mnt[:], 32, w=["rows0"])
+    dma("y", "u0", T.rows[8:16, :], T.u0[:], 32, w=["rows1"])
+    dma("s", "par", T.parb[:], T.par[:], 144, w=["parb"])
+    for h in early:
+        load_ac(h)
+    for c in range(NCH):
+        dma("y", "idm%d" % c, T.raw[:, CW * c:CW * c + CW], T.idm[:, CW * c:CW * c + CW], CW // 4, w=[RAWK[c]])
+        if c == 0:
+            dma("s", "ns0", T.ns[:], T.ns0[:], 32, w=["ns"])
+            dma("s", "e0", T.ev[:], T.e0[:], 32, w=["ev"])
+
+    names = ["a", "g", "h", "h2", "g48", "nb", "a16", "lt4", "e4", "e6", "cs", "cw", "wt", "lt2", "pb", "nb0"]
+    col = {n: T.cols[:, i:i + 1] for i, n in enumerate(names)}
+    iota(T.ip[:, 0:1], [[1, 1]], 0, 1, 1, ["ip"])
+    fill(T.onef[:], 1.0, 144, ["onef"])
+    fill(T.one[:], 1.0, 128, ["one"])
     ts(T.ip2[:, 0:1], T.ip[:, 0:1], 15, None, A.bitwise_and, r=["ip"], w=["ip20"])
     ts(T.ip2[:, 1:2], T.ip[:, 0:1], 4, None, A.arith_shift_right, r=["ip"], w=["ip21"])
-    tt(T.parl[:], T.parb[:], T.parh[:], A.subtract, r=["parb", "parh"], w=["parl"])
-    dma("y", "ph", T.part[0:128:16, :], T.parh[:], r=["parh"], w=["par", "q00", "q01", "q10", "q11"])
-    dma("y", "plo", T.part[1:128:16, :], T.parl[:], r=["parl"], w=["parx"])
-    dma("y", "ac", T.acs[:, PC:K], T.ac[:, PC:K], w=["acs"])
-    cp(T.cols[:, 0:2], T.ip2[:, 0:2], r=["ip20", "ip21"], w=["cols"])
-    ts(T.ia2[:], T.ia[:], 4, 7, A.arith_shift_right, A.bitwise_and, r=["ia"], w=["ia2"])
-    op("v", lambda: V.memset(T.zw[:], 0.0), w=["zw"])
-    pcol, gcol, kcol = T.cols[:, 0:1], T.cols[:, 1:2], T.cols[:, 2:3]
-    ts(T.oh[:], T.iv[:], pcol, None, A.is_equal, r=["iv", "cols"], w=["oh"])
-    ts(T.bw[:], T.ia2[:], gcol, None, A.is_equal, r=["ia2", "cols"], w=["bw"])
-    ts(kcol, pcol, 16.0, 512.0, A.add, A.mult, r=["cols"], w=["kcol"])
-    ncol = T.cols[:, 3:4]
-    ts(ncol, pcol, -1.0, None, A.mult, r=["cols"], w=["ncol"])
-    cp(T.zw[:, 0:160:16], T.bw[:, 0:160:16], r=["bw"], w=["zw"])
-    cp(T.moff[:], pb[6][:, 0:64], w=["moff"], x=["b6"])
-    ts(T.uoff[:], pb[7][:, 0:64], 1.0 / 512, None, A.mult, w=["uoff"], x=["b7"])
-    ts(T.ib2[:], T.ib[:], 127, None, A.bitwise_and, r=["ib"], w=["ib2"])
-    ts(T.iw[:], T.ib2[:], 0.0, None, A.is_equal, r=["ib2"], w=["iw"])
+    ts(T.ip2[:, 2:3], T.ip[:, 0:1], 1, None, A.arith_shift_right, r=["ip"], w=["ip22"])
+    fill(T.part[:, 0:W - PF], -65.0, (W - PF) // 2, ["pf0"])
+    cp(T.cols[:, 0:3], T.ip2[:, 0:3], r=["ip20", "ip21", "ip22"], w=["cols"])
+    fill(T.part[:, W - PF:PF], -65.0, PF - W // 2, ["pf1"])
+    iota(T.nn[:], [[1, 3], [0, RADIX]], 0, 3, 288, ["nn"], True)
+    where(T.zm[:], T.onef[:], [[1, 144]], -16, -16, 144, ["onef"], ["zm"])
+    iota(T.dg2[:], [[0, 3], [1, RADIX]], 0, 0, 288, ["dg2"], True)
+    iota(T.ia[:], [[0, 2], [1, 8], [0, 16]], 0, 0, 256, ["ia"])
+    where(T.zb[:], T.one[0:16, 0:128], [[1, 8], [0, 16]], 8, -1, 128, ["one"], ["zb"])
+    where(T.iw[:], T.one[:], [[0, 2], [-1, 128]], 0, 1, 256, ["one"], ["iw"])
+    iota(T.ib[:], [[1, 64], [0, 2]], 0, 0, 128, ["ib"])
 
-    def xgather(e, h):
-        src = T.oh[:, 0:16].indirect(T.uoff[:, L[h]])
-        if e == "s":
-            act(T.x[:, H[h]], src, F.Copy, r=["oh", "uoff"], w=["x%d" % h])
-        else:
-            cp(T.x[:, H[h]], src, r=["oh", "uoff"], w=["x%d" % h])
-
-    def mtab(t, e, h):
-        ms = T["ms%d" % t]
-        src = T.tab[:, 0:W].indirect(T.moff[:, L[h]])
-        key = "ms%d%d" % (t, h)
-        if e == "s":
-            act(ms[:, H[h]], src, F.Relu, r=TABK + ["moff"], w=[key], bias=DELTA[t])
-        else:
-            ts(ms[:, H[h]], src, DELTA[t], 0.0, A.add, A.max, r=TABK + ["moff"], w=[key])
-        send(dst_of[t], T["ml%d" % t][:, H[h]], ms[:, H[h]], "am%d%d" % (t, h), [key], False)
-
-    xgather("s", 1)
-    ts(T.im[:], T.iw[:], -1.0, None, A.mult, r=["iw"], w=["im"])
-    mtab(0, "v", 0)
-    mtab(0, "s", 1)
+    act(col["g48"], col["g"], F.Copy, r=["cols"], w=["g48"], scale=-48.0)
+    act(T.part[:, PF:W], T.part[:, 0:W - PF], F.Copy, W - PF, r=["pf0"], w=["pf2"])
+    act(T.dg3[:], T.nn[:], F.Identity, 288, r=["nn", "g48"], w=["dg3"], bias=col["g48"])
+    cp(T.rowf[:], T.rows[:], K, r=["rows0", "rows1"], w=["rowf"])
+    extract(pb[6][:, 0:64], T.zm, 16, T.rowf, True, True, ["zm", "rowf"], ["b6"], np_=16)
+    ts(T.dg1[:], T.parb[:], 1.0 / RADIX, 128.505, A.mult, A.add, n=288, r=["parb"], w=["dg1"])
+    act(T.du[:], T.dg1[:], F.Identity, 288, r=["dg1"], w=["du"], scale=-float(RADIX), bias=129.0 * (RADIX + 1))
+    act(T.rowb[:], T.rowf[:], F.Copy, K, r=["rowf"], w=["rowb"])
+    ts(T.bw[:], T.ia[:], col["g"], None, A.is_equal, n=256, r=["ia", "cols"], w=["bw"])
+    fill(T.zw[:], 0.0, 128, ["zw"])
+    tt(T.dg0[:], T.parb[:], T.du[:], A.add, 576, r=["parb", "du"], w=["dg0"])
+    for i in (3, 2, 1, 0):
+        dma("y", "dg%d" % i, T.part[2 * i:128:16, :], T["dg%d" % i][:], 72, r=["dg%d" % i],
+            w=[PD[i], "pf0", "pf1", "pf2"] if i == 3 else [PD[i]])
+    for h in early:
+        ac_abroad(h, ["dg0"])
+    for h in range(2):
+        if h not in early:
+            load_ac(h)
+    act(col["nb"], col["a"], F.Identity, r=["cols"], w=["nb"], scale=-128.0, bias=-128.0)
+    act(col["nb0"], col["a"], F.Copy, r=["cols"], w=["nb0"], scale=-128.0)
+    act(col["a16"], col["a"], F.Identity, r=["cols"], w=["a16"], bias=16.0)
+    for h in range(2):
+        mm([(pb[h][:], T.zb[:], T.rowb[:, H[h]], True, True)], 512, ["zb", "rowb"], ["b%d" % h])
+        ts(T.x[:, H[h]], pb[h][:], col["a"], None, A.is_equal, n=512, r=["cols"], w=["x%d" % h], x=["b%d" % h])
     cp(T.noff[:], T.ns[:], r=["ns"], w=["noff"])
-    xgather("s", 0)
-    cp(T.eoff[:], T.ev[:], r=["ev", "ev2"], w=["eoff"])
+    cp(T.eh[:], T.ev[:], r=["ev"], w=["eh"])
+    cp(T.zw[:, 0:256:16], T.bw[:, 0:256:16], r=["bw"], w=["zw"])
+    ts(col["lt4"], col["a"], 4.0, 0.5, A.is_lt, A.mult, r=["cols"], w=["lt4"])
+    ts(col["lt2"], col["a"], 2.0, 1.0 - RADIX, A.is_lt, A.mult, r=["cols"], w=["lt2"])
+    cp(T.moff[:], pb[6][:, 0:64], w=["moff"], x=["b6"])
+    ts(col["wt"], col["lt4"], 2.0 * RADIX, col["lt2"], A.mult, A.add, r=["lt4", "lt2"], w=["wt"])
+    for c in range(NCH):
+        lift("s" if c == 1 else "v", c)
+    for h in range(2):
+        mtab(0, h)
+    for h in (0, 1):
+        if not far0:
+            send(dst_of[0], T.ac0[:, H[h]], T.acs[:, H[h]], "aa0%d" % h, ["acs%d" % h], True)
+        if h not in early:
+            ac_abroad(h)
+    ac_arrives(0, PLAN["ac"])
+    act(T.zp[:], T.zw[:], F.Copy, 256, r=["zw", "wt"], w=["zp"], scale=col["wt"])
+    act(T.iwf[:], T.iw[:], F.Copy, 256, r=["iw"], w=["iwf"])
+    act(T.bx[:], T.bw[:, 112:240], F.Copy, 128, r=["bw"], w=["bx"], scale=-1.0)
+    act(T.xw2[:], T.iw[:, 16:144], F.Copy, 128, r=["iw"], w=["xw2"], scale=2.0)
+    act(col["h2"], col["h"], F.Identity, r=["cols"], w=["h2"], bias=-2.0)
+    act(T.bm[:], T.bw[:, 16:144], F.Copy, 128, r=["bw"], w=["bm"], scale=-64.0)
+    act(T.bp[:], T.bw[:, 16:144], F.Copy, 128, r=["bw"], w=["bp"], scale=64.0)
+    act(T.zn[:, 0:144], T.zw[:, 0:144], F.Copy, 144, r=["zw"], w=["zn"], scale=-1.0)
+    act(col["pb"], col["lt4"], F.Copy, r=["lt4"], w=["pbias"], scale=-64.0)
+    act(T.zk[:, 0:144], T.zw[:, 0:144], F.Copy, 144, r=["zw", "a16"], w=["zk"], scale=col["a16"])
+    act(T.zr[:], T.zw[:], F.Copy, 256, r=["zw", "cols"], w=["zr"], scale=col["a"])
+    ts(col["e4"], col["a"], 4.0, 0.5, A.is_equal, A.mult, r=["cols"], w=["e4"])
+    ts(col["e6"], col["a"], 6.0, 0.5, A.is_equal, A.mult, r=["cols"], w=["e6"])
+    fill(T.wf[:], 0.0, 64, ["wf"])
+    tt(col["cs"], col["e4"], col["e6"], A.add, r=["e4", "e6"], w=["cs"])
+    tt(T.xw[:], T.bw[:, 16:144], T.xw2[:], A.subtract, 256, r=["xw2", "bw"], w=["xw"])
+    ts(col["cw"], col["cs"], 2.0, col["lt4"], A.mult, A.add, r=["lt4", "cs"], w=["cw"])
+    ts(T.ws[:], T.ib[:], col["h2"], col["cs"], A.is_equal, A.mult, n=128, r=["ib", "h2", "cs"], w=["ws"])
+    ts(T.wo[:], T.ib[:], col["h"], col["cw"], A.is_equal, A.mult, n=128, r=["ib", "cols", "cw"], w=["wo"])
+    for b in (1, 3):
+        act(T.wo[:, b:128:16], T.wo[:, b:128:16], F.Copy, r=["wo"], w=["wo"], scale=-1.0)
+        act(T.wf[:, b:128:16], T.bw[:, 16 + b:144:16], F.Copy, r=["bw", "wf"], w=["wf%d" % b], scale=128.0)
 
-    def send_ac():
-        if far0:
-            ts(T.acu[:, PC:K], T.acs[:, PC:K], float(K), None, A.add, r=["acs"], w=["acu"])
-            send(dst_of[0], T.acl[:, PC:K], T.acu[:, PC:K], "aa0", ["acu"], True)
-        else:
-            ts(T.acq[:, PC:K], T.acs[:, PC:K], float(K), None, A.add, r=["acs"], w=["acq"])
-            send(dst_of[0], T.ac0[:, PC:K], T.acq[:, PC:K], "aa0", ["acq"], True)
-            send(dst_of[1], T.ac1[:], T.acq[:], "aa1", ["acq", "acqp"], True)
-        op("g", lambda: g.iota(T.ee[:], [[0, 16], [0, 130]], 0, 0, allow_small_or_imprecise_dtypes=True), w=["ee"])
-
-    def late_constants():
-        act(T.bm[:], T.bw[:], F.Copy, r=["bw"], w=["bm"], scale=-64.0)
-        act(T.xw2[:], T.iw[:, 16:144], F.Copy, r=["iw"], w=["xw2"], scale=2.0)
-        tt(T.xw[:], T.bw[:, 32:160], T.xw2[:], A.subtract, r=["xw2", "bw"], w=["xw"])
-        act(T.zk[:], T.zw[:], F.Copy, r=["zw", "kcol"], w=["zk"], scale=kcol)
-        if far0:
-            ts(T.acq[:, PC:K], T.acs[:, PC:K], float(K), None, A.add, r=["acs"], w=["acq"])
-            send(dst_of[2], T.ac2[:], T.acq[:], "aa2", ["acq", "acqp"], True)
-        for rg in range(2):
-            c0 = BASE + K * rg
-            mm([(pb[7][:, 64 * rg:64 * rg + 64], T.zw[:, 16 - k:144 - k], T.part[:, c0 + k:c0 + K:16], k == 0, k == 15)
-                for k in range(16)], ["zw"] + PARK, ["b7"])
-        for rg in range(2):
-            act(T["op%d" % rg][:], pb[7][:, 64 * rg:64 * rg + 64], F.Copy, w=["op%d" % rg], x=["b7"])
-
-    def hand_on():
-        for t in range(1, 3):
-            for q in range(N):
-                if q != rank and ac_sender(q, t) == rank:
-                    mine = [s for s in range(3) if src_of[s] == q][0]
-                    send((q - 1 - t) % N, T["ac%d" % t][:], T["ac%d" % mine][:], "aa%d" % t, ["ac%d" % mine, "ac0p"], True)
-
-    def new_e(step):
-        if step == 0:
-            tt(T.me[:], pb[7][:, 0:64], T.ev[:], A.max, r=["ev", "ev2"], w=["me"], x=["b7"])
-        elif step == 1:
-            ts(T.ev[:], T.me[:], K - 1, None, A.bitwise_and, r=["me"], w=["ev"])
-        elif step == 2:
-            cp(T.eoff[:], T.ev[:], r=["ev"], w=["eoff"])
-        else:
-            cp(T.fine[:], T.ev[:], r=["ev"], w=["fine"])
-
-    B, Bha = T.bw[:, 16:144], T.bw[:, 0:128]
-    Up, Kp = pb[6][:, 64:128], pb[2][:, 0:64]
+    I, B, Bha, Iah = T.iw[:, 0:128], T.bw[:, 0:128], T.bw[:, 112:240], T.iw[:, 16:144]
+    Up, Nf, Ep = pb[6][:, 0:64], pb[6][:, 64:128], pb[6][:, 128:192]
+    Ap, Er = pb[7][:, 0:64], pb[7][:, 128:192]
     MK, Y3 = ["mk0", "mk1"], ["y30", "y31"]
+
+    def half(b, wt, src, first, final, r):
+        mm([(pb[b][:], wt, src, first, final)], 512, r, ["b%d" % b])
 
     for t in range(RO):
         last = t == RO - 1
         rg = t % 2
         S0 = BASE + K * rg
-        ml, ac, ack = T["ml%d" % t], T["ac%d" % (t % 3)], "ac%d" % (t % 3)
-        act(T.p1[:], T.part[:, 0:W].indirect(T.noff[:, 0:64]), F.Copy, r=PARK + ["noff"], w=["p1"])
+        ml, ac = T["ml%d" % t], T["ac%d" % (t % 3)]
+        R = [slice(S0, S0 + 512), slice(S0 + 512, S0 + K)]
+        win, keys = (T.raw, RAWK) if t == 0 else (T.tab, TABK)
+        act(T.p1[:], T.part[:, 0:W].indirect(T.noff[:, 0:64]), F.Copy, 2 * GA - 64, r=PARK + ["noff"], w=["p1"])
+        extract(Up, T.zp, 128, T.p1, True, True, ["zp", "p1"], ["b6"])
+        ts(T.n1off[:], Up, UPC, None, A.add, w=["n1off"], x=["b6"])
+        act(T.dsn[:], Up, F.Identity, w=["dsn"], x=["b6"], bias=UPC - S0)
+        mm([(Er, T.iwf[:, 112:240], T.eh[:], True, True)], 256, ["iwf", "eh"], ["b7"])
+        cp(T.eoff[:], Er, w=["eoff"], x=["b7"])
+        for h in range(2):
+            b, hs = ["b%d" % (2 + h)], str(h)
+            tt(T.y1[:, H[h]], win[:, 0:W].indirect(T.noff[:, L[h]]), T.x[:, H[h]], A.mult, GA, r=keys + ["noff", "x" + hs], w=["y1" + hs])
+            half(2 + h, B, T.y1[:, H[h]], True, True, ["bw", "y1" + hs])
+            act(T.xx[:, H[h]], pb[2 + h][:], F.Abs, 512, r=["nb", "nb0"], w=["xx" + hs], x=b, scale=128.0,
+                bias=col["nb0" if t == 0 else "nb"])
+            half(2 + h, T.bx[:], T.xx[:, H[h]], True, False, ["bx", "xx" + hs])
+            tt(T.y2[:, H[h]], T.tab[:, 0:W].indirect(T.n1off[:, L[h]]), T.xx[:, H[h]], A.max, GA,
+               r=TABK + ["n1off", "xx" + hs], w=["y2" + hs])
+            half(2 + h, Bha, T.y2[:, H[h]], False, True, ["bw", "y2" + hs])
+        for h in range(2):
+            hs = str(h)
+            act(T.z[:, H[h]], ml[:, 0:K].indirect(T.eoff[:, L[h]]), F.Identity, GA,
+                r=["ml%d0" % t, "ml%d1" % t, "eoff"], w=["z" + hs], bias=HOLE[t])
+            tt(T.mk[:, H[h]], pb[2 + h][:], T.z[:, H[h]], A.is_equal, 512, r=["z" + hs], w=["mk" + hs], x=["b%d" % (2 + h)])
         if not last:
             for h in range(2):
-                mm([(pb[4 + h][:], T.iw[:, 0:128], T.tab[:, S0 + 512 * h:S0 + 512 * h + 512], True, False)],
-                   ["iw", "t%d%d" % (rg, h)], ["b%d" % (4 + h)])
-        for h in (1, 0):
-            tt(T.y1[:, H[h]], T.tab[:, 0:W].indirect(T.noff[:, L[h]]), T.x[:, H[h]], A.mult,
-               r=TABK + ["noff", "x%d" % h], w=["y1%d" % h])
-            mm([(pb[2 + h][:], B, T.y1[:, H[h]], True, True)], ["bw", "y1%d" % h], ["b%d" % (2 + h)])
-            if t > 0 and h == 1:
-                tt(T.x[:, H[0]], pb[0][:], T.x[:, H[0]], A.is_lt, r=["x0"], w=["x0"], x=["b0"])
-            if t > 0:
-                new_e(1 - h)
-            if h == 0:
-                extract(Up, T.zw, 16, T.p1, True, True, ["zw", "p1"], ["b6"])
-            if not last:
-                mm([(pb[1 - h][:], T.im[:, 0:128], T.tab[:, S0 + 512 * (1 - h):S0 + 512 * (1 - h) + 512], True, False)],
-                   ["im", "t%d%d" % (rg, 1 - h)], ["b%d" % (1 - h)])
-        if t == 0:
-            send_ac()
-        act(T.r1[:, H[1]], pb[3][:], F.Abs, r=["ncol"], w=["r11"], x=["b3"], bias=ncol)
-        act(T.m1[:, H[1]], T.r1[:, H[1]], F.Relu, r=["r11"], w=["m11"], bias=1.0, scale=-8.0)
-        opk = "op%d" % t
-        if 0 < t < RO - 1:
-            tt(T.dn[:], T.ns[:], T[opk][:], A.subtract, r=["ns", opk], w=["dn"])
-        if t > 0:
-            new_e(2)
-        ts(T.m1[:, H[0]], pb[2][:], pcol, None, A.is_equal, r=["cols"], w=["m10"], x=["b2"])
-        cp(T.n1off[:], Up, w=["n1off"], x=["b6"])
-        cp(T.up[:], Up, w=["up"], x=["b6"])
-        for h in (1, 0):
-            mm([(pb[2 + h][:], Bha, T.m1[:, H[h]], True, False)], ["bw", "m1%d" % h], ["b%d" % (2 + h)])
-        if last:
-            extract(pb[4][:, 0:64], T.zk, 16, T.x, True, True, ["zk", "x0", "x1"], ["b4"], block=True)
-        for h in range(2):
-            tt(T.y2[:, H[h]], T.tab[:, 0:W].indirect(T.n1off[:, L[h]]), T.m1[:, H[h]], A.mult,
-               r=TABK + ["n1off", "m1%d" % h], w=["y2%d" % h])
-        ts(T.ds[:], Up, -1.0, float(S0 - K), A.mult, A.add, w=["ds"], x=["b6"])
-        if t == 0:
-            late_constants()
-            tt(T.dn[:], T.ns[:], T[opk][:], A.subtract, r=["ns", opk], w=["dn"])
-        for h in range(2):
-            act(T.z[:, H[h]], ml[:, 0:K].indirect(T.eoff[:, L[h]]), F.Identity,
-                r=["ml%d0" % t, "ml%d1" % t, "eoff"], w=["z%d" % h], bias=1.0 - DELTA[t])
-        for h in range(2):
-            mm([(pb[2 + h][:], Bha, T.y2[:, H[h]], False, True)], ["bw", "y2%d" % h], ["b%d" % (2 + h)])
-            if not last:
-                mm([(pb[h][:], T.iw[:, 16:144], T.z[:, H[h]], False, False)], ["iw", "z%d" % h], ["b%d" % h])
-        for h in range(2):
-            tt(T.mk[:, H[h]], pb[2 + h][:], T.z[:, H[h]], A.is_equal, r=["z%d" % h], w=["mk%d" % h], x=["b%d" % (2 + h)])
-            if not last:
-                mm([(pb[h][:], T.bm[:, 32:160], T.mk[:, H[h]], False, True)], ["bm", "mk%d" % h], ["b%d" % h])
-                act(T.r1[:, H[h]], pb[h][:], F.Abs, w=["r1%d" % h], x=["b%d" % h], bias=31.0)
-                mm([(pb[4 + h][:], T.iw[:, 16:144], T.z[:, H[h]], False, False)], ["iw", "z%d" % h], ["b%d" % (4 + h)])
-        if last:
-            extract(Kp, T.zk, 32, T.mk, True, True, ["zk"] + MK, ["b2"], block=True)
-            ts(T.ub[:], pb[4][:, 0:64], float(-BIG), None, A.add, w=["ub"], x=["b4"])
-            extract(pb[3][:, 0:64], T.zw, 32, T.mk, True, True, ["zw"] + MK, ["b3"])
-        else:
+                hs, tk, qk = str(h), "t%d%d" % (rg, h), "q%d%d" % (rg, h)
+                half(h, Iah, T.z[:, H[h]], True, False, ["iw", "z" + hs])
+                half(h, T.bm[:], T.mk[:, H[h]], False, True, ["bm", "mk" + hs])
+                act(T.aa[:, H[h]], pb[h][:], F.Identity, 512, w=["aa" + hs], x=["b" + hs], bias=64.0)
+                half(6 + h, I, T.tab[:, R[h]], True, False, ["iw", tk] + TC)
+                half(6 + h, T.bp[:], T.mk[:, H[h]], False, True, ["bp", "mk" + hs])
+                tt(T.tab[:, R[h]], pb[6 + h][:], T.aa[:, H[h]], A.min, 512, r=["aa" + hs], w=[tk], x=["b%d" % (6 + h)])
+                half(4 + h, T.wo[:], T.part[:, R[h]], True, False, ["wo", qk] + PD)
+                half(4 + h, T.ws[:], T.p1[:, H[h]], False, False, ["ws", "p1"])
+                half(4 + h, T.wf[:], T.mk[:, H[h]], False, True, ["wf1", "wf3", "mk" + hs])
+                act(T.part[:, R[h]], pb[4 + h][:], F.Abs, 512, r=["pbias"], w=[qk], x=["b%d" % (4 + h)], bias=col["pb"])
+                half(h, T.xw[:], T.mk[:, H[h]], True, True, ["xw", "mk" + hs])
+                tt(T.x[:, H[h]], pb[h][:], T.x[:, H[h]], A.is_lt, 512, r=["x" + hs], w=["x" + hs], x=["b" + hs])
             for h in range(2):
-                if h == 1:
-                    extract(Kp, T.zw, 32, T.mk, True, True, ["zw"] + MK, ["b2"])
-                mm([(pb[4 + h][:], T.im[:, 0:128], T.r1[:, H[h]], False, True)], ["im", "r1%d" % h], ["b%d" % (4 + h)])
-                act(T.tab[:, S0 + 512 * h:S0 + 512 * h + 512], pb[4 + h][:], F.Identity,
-                    w=["t%d%d" % (rg, h)], x=["b%d" % (4 + h)], scale=0.5, bias=15.5)
-        if t == 0:
-            ts(T.ee[:, :, 1:129:16], T.ic[:], 0.0, None, A.is_equal, r=["ic"], w=["ee"])
-        if t == 0 and far0_in:
-            cp(T.ac0[:, PC:K], T.acl[:, PC:K], r=["acl"], w=["ac0"])
-
-        def move(h):
-            tt(T.y3[:, H[h]], ac[:, 0:K].indirect(T.eoff[:, L[h]]), T.mk[:, H[h]], A.mult,
-               r=[ack, "ac0p", "eoff", "mk%d" % h], w=["y3%d" % h])
-        move(0)
-        if not last:
-            mtab(t + 1, "s", 0)
-            mtab(t + 1, "s", 1)
-            if t == 0 and far0_in:
-                hand_on()
-            move(1)
-            pn, pnk = (T.op2, "op2") if t == 0 else (T.pnx, "pnx")
-
-            def xsum(h):
-                mm([(pb[h][:], T.xw[:], T.mk[:, H[h]], True, True)], ["xw", "mk%d" % h], ["b%d" % h])
-            xsum(1)
-            extract(pb[6][:, 0:64], T.zw, 32, T.y3, True, True, ["zw"] + Y3, ["b6"])
-            tt(T.tq[:], Kp, T.dn[:], A.mult, r=["dn"], w=["tq"], x=["b2"])
-            tt(T.tq2[:], Kp, T.ds[:], A.mult, r=["ds"], w=["tq2"], x=["b2"])
-            tt(pn[:], T.tq[:], T[opk][:], A.add, r=["tq", opk], w=[pnk])
-            cp(T.pnh[:], pn[:], r=[pnk], w=["pnh"])
-            tt(T.up2[:], T.tq2[:], T.up[:], A.add, r=["tq2", "up"], w=["up2"])
-            tt(T.pnl[:], pn[:], T.pnh[:], A.subtract, r=[pnk, "pnh"], w=["pnl"])
-            tt(T.ns[:], pb[6][:, 0:64], T.up2[:], A.add, r=["up2"], w=["ns"], x=["b6"])
-            for h in (1, 0):
-                it = []
-                for a in range(8):
-                    o = pb[2 + h][:, a:512:8]
-                    it.append((o, T.ee[:, 2 * a + h, 1:129], T.pnh[:], True, False))
-                    it.append((o, T.ee[:, 2 * a + h, 0:128], T.pnl[:], False, True))
-                mm(it, ["ee", "pnh", "pnl"], ["b%d" % (2 + h)])
-            xsum(0)
-            extract(pb[7][:, 0:64], T.zw, 16, T.y3, True, True, ["zw"] + Y3, ["b7"])
-            tt(T.x[:, H[1]], pb[1][:], T.x[:, H[1]], A.is_lt, r=["x1"], w=["x1"], x=["b1"])
-            cp(T.noff[:], T.ns[:], r=["ns"], w=["noff"])
-            cp(T.part[:, S0 + 1:S0 + K:2], pb[3][:], w=["q%d1" % rg], x=["b3"])
-            act(T.part[:, S0:S0 + K:2], pb[2][:], F.Copy, w=["q%d0" % rg], x=["b2"])
+                mtab(t + 1, h)
+            if t < 2:
+                hand_on(t + 1)
+                ac_arrives(t + 1, PLAN["push"])
         else:
-            move(1)
-            extract(pb[7][:, 0:64], T.zw, 16, T.y3, True, True, ["zw"] + Y3, ["b7"])
-            extract(pb[6][:, 0:64], T.zw, 32, T.y3, True, True, ["zw"] + Y3, ["b6"])
-            tt(T.um[:], Kp, T.ub[:], A.max, r=["ub"], w=["um"], x=["b2"])
-            tt(T.tq2[:], pb[3][:, 0:64], T.ds[:], A.mult, r=["ds"], w=["tq2"], x=["b3"])
-            ts(T.us[:], T.um[:], BIG - 1, None, A.bitwise_and, r=["um"], w=["us"])
-            tt(T.up2[:], T.tq2[:], T.up[:], A.add, r=["tq2", "up"], w=["up2"])
-            ts(T.finu[:], T.us[:], 1.0 / 512, None, A.mult, r=["us"], w=["finu"])
-            dma("s", "yu", T.yu[:], T.finu[:], r=["finu"])
-            new_e(0)
-            new_e(1)
-            tt(T.finn[:], pb[6][:, 0:64], T.up2[:], A.add, r=["up2"], w=["finn"], x=["b6"])
-            new_e(3)
-            dma("y", "yn", T.yn[:], T.finn[:], r=["finn"])
-            dma("s", "yea", T.ye[0:112, :], T.fine[16:128, :], r=["fine"])
-            dma("y", "yeb", T.ye[112:128, :], T.fine[0:16, :], r=["fine"])
+            extract(pb[4][:, 0:64], T.zr, 128, T.x, True, True, ["zr", "x0", "x1"], ["b4"], block=True)
+            act(T.ub[:], pb[4][:, 0:64], F.Copy, w=["ub"], x=["b4"])
+            extract(pb[5][:, 0:64], T.zk, 16, T.mk, True, True, ["zk"] + MK, ["b5"], block=True)
+            tt(T.um[:], pb[5][:, 0:64], T.ub[:], A.max, r=["ub"], w=["um"], x=["b5"])
+            ts(T.us[:], T.um[:], 15, None, A.bitwise_and, r=["um"], w=["us"])
+            cp(T.finu[:], T.us[:], r=["us"], w=["finu"])
+            dma("s", "yu", T.yu[:], T.finu[:], 32, r=["finu"])
+        for h in range(2):
+            tt(T.y3[:, H[h]], ac[:, 0:K].indirect(T.eoff[:, L[h]]), T.mk[:, H[h]], A.mult, GA,
+               r=ACK[t % 3] + ["eoff", "mk%d" % h], w=["y3%d" % h])
+        mm([(Nf, I, T.one[:, 0:64], True, False)], 64, ["iw", "one"], ["b6"])
+        extract(Nf, T.zn, 16, T.mk, False, True, ["zn"] + MK, ["b6"])
+        tt(T.tq[:], Nf, T.dsn[:], A.mult, r=["dsn"], w=["tq"], x=["b6"])
+        tt(T.te[:], Nf, T.eh[:], A.mult, r=["eh"], w=["te"], x=["b6"])
+        mm([(Ap, T.iwf[:, 0:128], T.tq[:], True, False)], 256, ["iwf", "tq"], ["b7"])
+        extract(Ap, T.zw, 16, T.y3, False, True, ["zw"] + Y3, ["b7"])
+        if not last:
+            ts(T.noff[:], Ap, float(S0), None, A.add, w=["noff"], x=["b7"])
+            mm([(Ep, I, T.te[:], True, False)], 64, ["iw", "te"], ["b6"])
+            extract(Ep, T.zw, 16, T.y3, False, True, ["zw"] + Y3, ["b6"])
+            act(T.eh[:], Ep, F.Copy, w=["eh"], x=["b6"])
+        else:
+            tt(T.td[:], T.te[:], T.tq[:], A.subtract, 128, r=["te", "tq"], w=["td"])
+            ts(T.finn[:], Ap, float(S0), None, A.add, w=["finn"], x=["b7"])
+            dma("y", "yn", T.yn[:], T.finn[:], 32, r=["finn"])
+            tt(T.fine[:], Ap, T.td[:], A.add, r=["td"], w=["fine"], x=["b7"])
+            dma("s", "ye", T.ye[:], T.fine[:], 32, r=["fine"])
 
-    for s, v in cnt.items():
+    Q = {"v": g.vector, "s": g.scalar, "p": g.tensor, "g": g, "y": g.sync}
+    total = {}
+    known = {e: {} for e in Q}
+    token = {}
+    before = hazards(calls)
+    for i in issue_order(calls):
+        c = calls[i]
+        e = c["e"]
+        if e == "dma":
+            token[i] = token[i - 1]
+            continue
+        if e == "-":
+            total[c["sem"][0]] = c["sem"][1]
+            token[i] = (c["sem"][0], c["sem"][1], {})
+            continue
+        toks = [token[j] for j in before[i] if j in token and not (e == "p" and calls[j]["e"] == "p")
+                and not (c["chain"] and c["chain"] == calls[j]["chain"] and not set(calls[j]["w"]) & set(c["r"] + c["w"]))]
+        for sem, val, clock in sorted(toks, key=lambda tk: -tk[1]):
+            if known[e].get(sem, 0) < val:
+                Q[e].wait_ge(T.sem[sem], val)
+                known[e][sem] = val
+            for s, v in clock.items():
+                known[e][s] = max(known[e].get(s, 0), v)
+        ins = c["fn"]()
+        if isinstance(c["sem"], tuple):
+            total["ls"] = total.get("ls", 0) + c["sem"][1]
+            continue
+        step = 16 if c["sem"][0] == "d" else 1
+        total[c["sem"]] = total.get(c["sem"], 0) + step
+        ins.then_inc(T.sem[c["sem"]], step)
+        token[i] = (c["sem"], total[c["sem"]], dict(known[e]))
+    for s, v in total.items():
         if known["g"].get(s, 0) < v:
             g.wait_ge(T.sem[s], v)

from concourse.mybir import AluOpType, ActivationFunctionType

A = AluOpType
F = ActivationFunctionType
BASE, K, W, RO = 2560, 1024, 4608, 4
HOLE = [0.25, 0.5, 0.75, 0.875]
NCH = 4
CW = W // NCH
PF = 3072
AC_EARLY = [1]
AC_NEAR = [0]
HELP = [0]
RADIX = 96
UPC = -64.0 * (RADIX + 1)
PUSH = ["sv", "ss", "ss", "ss"]
PLAN = dict(cyc=0.00087, pe=0.00044, gather=1.4, hop=0.2, issue=0.3, load0=1.6, load=0.0025, push=2.5, link=1.2, ac=3.0, rounds=6)

SCRATCH = {
    "raw": ("sbuf", [128, W], "bfloat16"),
    "tab": ("sbuf", [128, W], "bfloat16"),
    "part": ("sbuf", [128, W], "bfloat16"),
    "parb": ("sbuf", [128, 288], "int32"),
    "nn": ("sbuf", [128, 288], "float32"),
    "du": ("sbuf", [128, 288], "float32"),
    "rows": ("sbuf", [16, K], "int32"),
    "rowf": ("sbuf", [16, K], "float32"),
    "rowb": ("sbuf", [16, K], "bfloat16"),
    "acs": ("sbuf", [128, K], "int32"),
    "y3": ("sbuf", [128, K], "float16"),
    "ns": ("sbuf", [128, 64], "int32"),
    "ev": ("sbuf", [128, 64], "int32"),
    "um": ("sbuf", [128, 64], "int32"),
    "us": ("sbuf", [128, 64], "int32"),
    "te": ("sbuf", [128, 64], "float16"),
    "ip": ("sbuf", [128, 8], "int32"),
    "ip2": ("sbuf", [128, 8], "int32"),
    "cols": ("sbuf", [128, 16], "float32"),
    "ia": ("sbuf", [128, 256], "int32"),
    "ib": ("sbuf", [128, 128], "int32"),
    "onef": ("sbuf", [16, 144], "float32"),
    "zm": ("sbuf", [16, 144], "float32"),
    "zb": ("sbuf", [16, 128], "bfloat16"),
    "iwf": ("sbuf", [128, 256], "float32"),
}
for _n in ["x", "y1", "p1", "xx", "y2", "z", "mk", "aa"]:
    SCRATCH[_n] = ("sbuf", [128, K], "bfloat16")
for _n in ["moff", "noff", "n1off", "eoff"]:
    SCRATCH[_n] = ("sbuf", [128, 64], "uint16")
for _n in ["dsn", "tq", "td", "eh", "ub", "finn", "fine", "finu"]:
    SCRATCH[_n] = ("sbuf", [128, 64], "float32")
for _n in ["one", "bw", "iw", "zw", "zp", "zn", "zk", "zr"]:
    SCRATCH[_n] = ("sbuf", [128, 256], "bfloat16")
for _n in ["bm", "bp", "bx", "xw", "xw2", "wo", "ws", "wf"]:
    SCRATCH[_n] = ("sbuf", [128, 128], "bfloat16")
for _t in range(4):
    SCRATCH["dg%d" % _t] = ("sbuf", [128, 288], "bfloat16")
for _t in range(3):
    SCRATCH["ac%d" % _t] = ("sbuf", [128, K], "int32")
for _t in range(RO):
    SCRATCH["ms%d" % _t] = ("sbuf", [128, K], "bfloat16")
    SCRATCH["ml%d" % _t] = ("sbuf", [128, K], "bfloat16")
for _b in range(8):
    SCRATCH["pb%d" % _b] = ("psum", [128, 512], "float32")

DMAS = (["mnt", "u0", "ac0", "ac1", "par", "ns0", "e0", "yn", "ye", "yu"] + ["idm%d" % c for c in range(NCH)]
        + ["dg%d" % c for c in range(4)])
SEMAPHORES = (["cv", "cs", "cp", "cg", "ls", "aa00", "aa01", "aa10", "aa11", "aa20", "ah"] + ["d_" + n for n in DMAS]
              + ["am%d%d" % (t, h) for t in range(RO) for h in range(2)])


def hazards(calls):
    lastw, readers, prev, before = {}, {}, {}, []
    for i, c in enumerate(calls):
        d = set(c["after"])
        for k in c["r"] + c["w"] + c["x"]:
            if k in lastw:
                d.add(lastw[k])
        for k in c["w"]:
            d.update(readers.get(k, []))
        for k in c["x"]:
            d.update(j for j in readers.get(k, []) if calls[j]["e"] != c["e"])
        if c["chain"]:
            if c["chain"] in prev:
                d.add(prev[c["chain"]])
            prev[c["chain"]] = i
        for k in c["r"] + c["x"]:
            readers.setdefault(k, []).append(i)
        for k in c["w"]:
            lastw[k] = i
            readers[k] = []
        before.append(sorted(d))
    return before


def issue_order(calls):
    n = len(calls)
    before = hazards(calls)
    after = [[] for _ in calls]
    for i in range(n):
        for j in before[i]:
            after[j].append(i)

    def gap(j, i):
        if calls[j]["chain"] and calls[j]["chain"] == calls[i]["chain"]:
            return calls[j]["busy"]
        hop = 0.0 if calls[j]["e"] == calls[i]["e"] == "p" else PLAN["hop"]
        return calls[j]["busy"] + calls[j]["late"] + hop

    def place(order, back):
        taken, at = {}, [0.0] * n
        for i in order:
            busy = calls[i]["busy"]
            if back:
                s = max([calls[i]["late"]] + [at[k] + calls[k]["busy"] + gap(i, k) - busy for k in after[i]])
            else:
                s = max([0.0] + [at[j] + gap(j, i) for j in before[i]])
            line = taken.setdefault(calls[i]["e"], [])
            for a, b in line:
                if s + busy <= a:
                    break
                s = max(s, b)
            line.append((s, s + busy))
            line.sort()
            at[i] = s
        return at

    way = [0.0] * n
    for j in reversed(range(n)):
        way[j] = max([calls[j]["busy"] + calls[j]["late"]] + [gap(j, i) + way[i] for i in after[j]])
    at = place(sorted(range(n), key=lambda i: (-way[i], i)), False)
    best = None
    for _ in range(PLAN["rounds"]):
        end = max(at[i] + calls[i]["busy"] + calls[i]["late"] for i in range(n))
        if best is None or end < best[0]:
            best = (end, at)
        rev = place(sorted(range(n), key=lambda i: (-at[i] - calls[i]["busy"], -i)), True)
        at = place(sorted(range(n), key=lambda i: (-rev[i] - calls[i]["busy"], i)), False)
    PLAN["end"] = best[0]
    return sorted(range(n), key=lambda i: (best[1][i], i))


def rank_program(g, core, T, topo):
    rank = T.rank_of(core)
    cores = list(T.cores)
    N = len(cores)
    H = [slice(0, 512), slice(512, 1024)]
    L = [slice(0, 32), slice(32, 64)]

    def bits(engs):
        return sum(1 << i for i in engs)

    def same_chip(a, b):
        return cores[b] in topo.cores_of(cores[a])

    def helper(q):
        return [c for c in topo.cores_of(cores[q]) if c not in cores and topo.die(c) != topo.die(cores[q])][0]

    def spare(q):
        far = [d for d in range(N) if not same_chip(q, d)][0]
        return [i for i in topo.engines(cores[q], helper(q)) if i not in topo.engines(cores[q], cores[far])]

    def first_far(q):
        return [s for s in range(3) if not same_chip(q, (q - 1 - s) % N)][0]

    if rank is None:
        for q in range(N):
            if helper(q) == core and first_far(q) in HELP:
                s = first_far(q)
                d = cores[(q - 1 - s) % N]
                g.wait_ge(T.sem.ah, len(spare(q)))
                rid, pid = topo.addr(d, core)
                en = topo.engines(core, d)
                g.remote_dma(T["ac%d" % s][:, H[1]], T.acs[:, H[1]], T.sem["aa%d1" % s], T.sem.ls, pid, rid, bits(en))
                g.wait_ge(T.sem.ls, len(en))
        return

    calls = []

    def call(e, fn, sem, busy, r=(), w=(), x=(), late=0.0, chain=None, after=()):
        calls.append(dict(e=e, fn=fn, sem=sem, busy=busy, late=late, r=list(r), w=list(w), x=list(x), chain=chain, after=list(after)))
        return len(calls) - 1

    def op(e, fn, n, r=(), w=(), x=()):
        call(e, fn, "c" + e, n * PLAN["pe"] if e == "p" else max(n, 64) * PLAN["cyc"], r, w, x, chain="g" if e == "g" else None)

    def dma(e, name, out, in_, kib, r=(), w=()):
        q = {"s": g.scalar, "y": g.sync}[e]
        call(e, lambda: q.dma_start(out, in_), "d_" + name, 0.05, r, w, chain="dma" + e)
        call("dma", None, None, kib * PLAN["load"], (), w, late=PLAN["load0"], chain="dma", after=[len(calls) - 1])

    def lanes(src, dst, sp):
        return spare(src) if sp and same_chip(src, dst) else topo.engines(cores[src], cores[dst])

    def write(to, en, out, in_, sem, r):
        rid, pid = topo.addr(to, core)
        call("g", lambda: g.remote_dma(out, in_, T.sem[sem], T.sem.ls, pid, rid, bits(en)), ("ls", len(en)), PLAN["issue"], r, chain="g")

    def send(dst, out, in_, sem, r, sp):
        write(cores[dst], lanes(rank, dst, sp), out, in_, sem, r)

    def arrives(key, sem, src, sp, late, busy=0.001):
        call("-", None, (sem, len(lanes(src, rank, sp))), busy, w=[key], late=late, after=[len(calls) - 1])

    def mm(items, n, r, w):
        def fn():
            ins = None
            for (o, l, rh, st, sp) in items:
                ins = g.tensor.matmul(o, l, rh, st, sp)
            return ins
        op("p", fn, n, r=r, w=w)

    def extract(out, wt, off, src, first, last, r, w, block=False, np_=128):
        it = []
        for k in range(16):
            rh = src[0:np_, 64 * k:64 * k + 64] if block else src[0:np_, k:K:16]
            it.append((out, wt[0:np_, off - k:off - k + 128], rh, first and k == 0, last and k == 15))
        mm(it, K if np_ == 128 else 4 * K, r, w)

    V, S = g.vector, g.scalar
    pb = [T["pb%d" % b] for b in range(8)]
    TC = ["tc%d" % c for c in range(NCH)]
    RAWK = ["raw%d" % c for c in range(NCH)]
    TABK = TC + ["t00", "t01", "t10", "t11"]
    PD = ["pd%d" % c for c in range(4)]
    PARK = PD + ["q00", "q01", "q10", "q11"]
    src_of = [(rank + 1 + t % 3) % N for t in range(RO)]
    dst_of = [(rank - 1 - t % 3) % N for t in range(RO)]
    far0 = not same_chip(rank, dst_of[0])
    GA = int(64 + 512 * PLAN["gather"])

    def ts(out, in0, s1, s2, o0, o1=None, n=64, r=(), w=(), x=()):
        if o1 is None:
            op("v", lambda: V.tensor_scalar(out, in0, s1, None, o0), n, r, w, x)
        else:
            op("v", lambda: V.tensor_scalar(out, in0, s1, s2, o0, o1), n, r, w, x)

    def tt(out, in0, in1, o, n=64, r=(), w=(), x=()):
        op("v", lambda: V.tensor_tensor(out, in0, in1, o), n, r, w, x)

    def cp(out, in_, n=64, r=(), w=(), x=()):
        op("v", lambda: V.tensor_copy(out, in_), n, r, w, x)

    def fill(ap, c, n, w):
        op("v", lambda: V.memset(ap, c), n, w=w)

    def act(out, in_, f, n=64, r=(), w=(), x=(), **kw):
        op("s", lambda: S.activation(out, in_, f, **kw), n, r, w, x)

    def iota(out, pattern, base, cm, n, w, small=False):
        op("g", lambda: g.iota(out, pattern, base, cm, allow_small_or_imprecise_dtypes=small), 150 + 2 * n, w=w)

    def where(out, in_, pattern, base, cm, n, r, w):
        op("g", lambda: g.affine_select(out, in_, pattern, A.is_equal, 0.0, base, cm), 200 + 2 * n, r=r, w=w)

    def ac_sender(q, t):
        d = (q - 1 - t) % N
        if same_chip(q, d):
            return q
        return q if first_far(q) == t else (q - 1 - first_far(q)) % N

    ACK = [["ac%d%d" % (t, h) for h in range(2 if t == 0 or first_far(src_of[t]) == t else 1)] for t in range(3)]

    def ac_arrives(t, late):
        for k in ACK[t]:
            arrives(k, "aa" + k[2:], ac_sender(src_of[t], t), True, late)

    def lift(e, c):
        sl = slice(CW * c, CW * c + CW)
        if e == "s":
            act(T.tab[:, sl], T.raw[:, sl], F.Identity, CW, r=[RAWK[c]], w=[TC[c]], bias=1.0)
        else:
            ts(T.tab[:, sl], T.raw[:, sl], 1.0, None, A.add, n=CW // 2, r=[RAWK[c]], w=[TC[c]])

    def load_ac(h):
        dma("y", "ac%d" % h, T.acs[:, H[h]], T.ac[:, H[h]], 256, w=["acs%d" % h])

    def ac_abroad(h, r=()):
        ff = first_far(rank)
        if h == 1 and ff in HELP:
            write(helper(rank), spare(rank), T.acs[:, H[1]], T.acs[:, H[1]], "ah", ["acs1"] + list(r))
        else:
            send(dst_of[ff], T["ac%d" % ff][:, H[h]], T.acs[:, H[h]], "aa%d%d" % (ff, h), ["acs%d" % h] + list(r), True)

    def hand_on(t):
        for q in range(N):
            if q != rank and ac_sender(q, t) == rank:
                mine = src_of.index(q)
                send((q - 1 - t) % N, T["ac%d" % t][:], T["ac%d" % mine][:], "aa%d0" % t, ACK[mine], True)
        if far0 and t == 1:
            send(dst_of[2], T.ac2[:], T.acs[:], "aa20", ["acs0", "acs1"], True)

    def mtab(t, h):
        ms = T["ms%d" % t]
        win, keys, sh = (T.raw, RAWK, 1.0) if t == 0 else (T.tab, TABK, 0.0)
        src = win[:, 0:W].indirect(T.moff[:, L[h]])
        key = "ms%d%d" % (t, h)
        if PUSH[t][h] == "s":
            act(ms[:, H[h]], src, F.Relu, GA, r=keys + ["moff"], w=[key], bias=sh - HOLE[t])
        else:
            ts(ms[:, H[h]], src, sh - HOLE[t], 0.0, A.add, A.max, n=GA, r=keys + ["moff"], w=[key])
        send(dst_of[t], T["ml%d" % t][:, H[h]], ms[:, H[h]], "am%d%d" % (t, h), [key], False)
        arrives("ml%d%d" % (t, h), "am%d%d" % (t, h), src_of[t], False, PLAN["push"], PLAN["link"])

    early = AC_EARLY if far0 else AC_NEAR
    dma("s", "mnt", T.rows[0:8, :], T.mnt[:], 32, w=["rows0"])
    dma("y", "u0", T.rows[8:16, :], T.u0[:], 32, w=["rows1"])
    dma("s", "par", T.parb[:], T.par[:], 144, w=["parb"])
    for h in early:
        load_ac(h)
    for c in range(NCH):
        dma("y", "idm%d" % c, T.raw[:, CW * c:CW * c + CW], T.idm[:, CW * c:CW * c + CW], CW // 4, w=[RAWK[c]])
        if c == 0:
            dma("s", "ns0", T.ns[:], T.ns0[:], 32, w=["ns"])
            dma("s", "e0", T.ev[:], T.e0[:], 32, w=["ev"])

    names = ["a", "g", "h", "h2", "g48", "nb", "a16", "lt4", "e4", "e6", "cs", "cw", "wt", "lt2", "pb", "nb0"]
    col = {n: T.cols[:, i:i + 1] for i, n in enumerate(names)}
    iota(T.ip[:, 0:1], [[1, 1]], 0, 1, 1, ["ip"])
    fill(T.onef[:], 1.0, 144, ["onef"])
    fill(T.one[:], 1.0, 128, ["one"])
    ts(T.ip2[:, 0:1], T.ip[:, 0:1], 15, None, A.bitwise_and, r=["ip"], w=["ip20"])
    ts(T.ip2[:, 1:2], T.ip[:, 0:1], 4, None, A.arith_shift_right, r=["ip"], w=["ip21"])
    ts(T.ip2[:, 2:3], T.ip[:, 0:1], 1, None, A.arith_shift_right, r=["ip"], w=["ip22"])
    fill(T.part[:, 0:W - PF], -65.0, (W - PF) // 2, ["pf0"])
    cp(T.cols[:, 0:3], T.ip2[:, 0:3], r=["ip20", "ip21", "ip22"], w=["cols"])
    fill(T.part[:, W - PF:PF], -65.0, PF - W // 2, ["pf1"])
    iota(T.nn[:], [[1, 3], [0, RADIX]], 0, 3, 288, ["nn"], True)
    where(T.zm[:], T.onef[:], [[1, 144]], -16, -16, 144, ["onef"], ["zm"])
    iota(T.dg2[:], [[0, 3], [1, RADIX]], 0, 0, 288, ["dg2"], True)
    iota(T.ia[:], [[0, 2], [1, 8], [0, 16]], 0, 0, 256, ["ia"])
    where(T.zb[:], T.one[0:16, 0:128], [[1, 8], [0, 16]], 8, -1, 128, ["one"], ["zb"])
    where(T.iw[:], T.one[:], [[0, 2], [-1, 128]], 0, 1, 256, ["one"], ["iw"])
    iota(T.ib[:], [[1, 64], [0, 2]], 0, 0, 128, ["ib"])

    act(col["g48"], col["g"], F.Copy, r=["cols"], w=["g48"], scale=-48.0)
    act(T.part[:, PF:W], T.part[:, 0:W - PF], F.Copy, W - PF, r=["pf0"], w=["pf2"])
    act(T.dg3[:], T.nn[:], F.Identity, 288, r=["nn", "g48"], w=["dg3"], bias=col["g48"])
    cp(T.rowf[:], T.rows[:], K, r=["rows0", "rows1"], w=["rowf"])
    extract(pb[6][:, 0:64], T.zm, 16, T.rowf, True, True, ["zm", "rowf"], ["b6"], np_=16)
    ts(T.dg1[:], T.parb[:], 1.0 / RADIX, 128.505, A.mult, A.add, n=288, r=["parb"], w=["dg1"])
    act(T.du[:], T.dg1[:], F.Identity, 288, r=["dg1"], w=["du"], scale=-float(RADIX), bias=129.0 * (RADIX + 1))
    act(T.rowb[:], T.rowf[:], F.Copy, K, r=["rowf"], w=["rowb"])
    ts(T.bw[:], T.ia[:], col["g"], None, A.is_equal, n=256, r=["ia", "cols"], w=["bw"])
    fill(T.zw[:], 0.0, 128, ["zw"])
    tt(T.dg0[:], T.parb[:], T.du[:], A.add, 576, r=["parb", "du"], w=["dg0"])
    for i in (3, 2, 1, 0):
        dma("y", "dg%d" % i, T.part[2 * i:128:16, :], T["dg%d" % i][:], 72, r=["dg%d" % i],
            w=[PD[i], "pf0", "pf1", "pf2"] if i == 3 else [PD[i]])
    for h in early:
        ac_abroad(h, ["dg0"])
    for h in range(2):
        if h not in early:
            load_ac(h)
    act(col["nb"], col["a"], F.Identity, r=["cols"], w=["nb"], scale=-128.0, bias=-128.0)
    act(col["nb0"], col["a"], F.Copy, r=["cols"], w=["nb0"], scale=-128.0)
    act(col["a16"], col["a"], F.Identity, r=["cols"], w=["a16"], bias=16.0)
    for h in range(2):
        mm([(pb[h][:], T.zb[:], T.rowb[:, H[h]], True, True)], 512, ["zb", "rowb"], ["b%d" % h])
        ts(T.x[:, H[h]], pb[h][:], col["a"], None, A.is_equal, n=512, r=["cols"], w=["x%d" % h], x=["b%d" % h])
    cp(T.noff[:], T.ns[:], r=["ns"], w=["noff"])
    cp(T.eh[:], T.ev[:], r=["ev"], w=["eh"])
    cp(T.zw[:, 0:256:16], T.bw[:, 0:256:16], r=["bw"], w=["zw"])
    ts(col["lt4"], col["a"], 4.0, 0.5, A.is_lt, A.mult, r=["cols"], w=["lt4"])
    ts(col["lt2"], col["a"], 2.0, 1.0 - RADIX, A.is_lt, A.mult, r=["cols"], w=["lt2"])
    cp(T.moff[:], pb[6][:, 0:64], w=["moff"], x=["b6"])
    ts(col["wt"], col["lt4"], 2.0 * RADIX, col["lt2"], A.mult, A.add, r=["lt4", "lt2"], w=["wt"])
    for c in range(NCH):
        lift("s" if c == 1 else "v", c)
    for h in range(2):
        mtab(0, h)
    for h in (0, 1):
        if not far0:
            send(dst_of[0], T.ac0[:, H[h]], T.acs[:, H[h]], "aa0%d" % h, ["acs%d" % h], True)
        if h not in early:
            ac_abroad(h)
    ac_arrives(0, PLAN["ac"])
    act(T.zp[:], T.zw[:], F.Copy, 256, r=["zw", "wt"], w=["zp"], scale=col["wt"])
    act(T.iwf[:], T.iw[:], F.Copy, 256, r=["iw"], w=["iwf"])
    act(T.bx[:], T.bw[:, 112:240], F.Copy, 128, r=["bw"], w=["bx"], scale=-1.0)
    act(T.xw2[:], T.iw[:, 16:144], F.Copy, 128, r=["iw"], w=["xw2"], scale=2.0)
    act(col["h2"], col["h"], F.Identity, r=["cols"], w=["h2"], bias=-2.0)
    act(T.bm[:], T.bw[:, 16:144], F.Copy, 128, r=["bw"], w=["bm"], scale=-64.0)
    act(T.bp[:], T.bw[:, 16:144], F.Copy, 128, r=["bw"], w=["bp"], scale=64.0)
    act(T.zn[:, 0:144], T.zw[:, 0:144], F.Copy, 144, r=["zw"], w=["zn"], scale=-1.0)
    act(col["pb"], col["lt4"], F.Copy, r=["lt4"], w=["pbias"], scale=-64.0)
    act(T.zk[:, 0:144], T.zw[:, 0:144], F.Copy, 144, r=["zw", "a16"], w=["zk"], scale=col["a16"])
    act(T.zr[:], T.zw[:], F.Copy, 256, r=["zw", "cols"], w=["zr"], scale=col["a"])
    ts(col["e4"], col["a"], 4.0, 0.5, A.is_equal, A.mult, r=["cols"], w=["e4"])
    ts(col["e6"], col["a"], 6.0, 0.5, A.is_equal, A.mult, r=["cols"], w=["e6"])
    fill(T.wf[:], 0.0, 64, ["wf"])
    tt(col["cs"], col["e4"], col["e6"], A.add, r=["e4", "e6"], w=["cs"])
    tt(T.xw[:], T.bw[:, 16:144], T.xw2[:], A.subtract, 256, r=["xw2", "bw"], w=["xw"])
    ts(col["cw"], col["cs"], 2.0, col["lt4"], A.mult, A.add, r=["lt4", "cs"], w=["cw"])
    ts(T.ws[:], T.ib[:], col["h2"], col["cs"], A.is_equal, A.mult, n=128, r=["ib", "h2", "cs"], w=["ws"])
    ts(T.wo[:], T.ib[:], col["h"], col["cw"], A.is_equal, A.mult, n=128, r=["ib", "cols", "cw"], w=["wo"])
    for b in (1, 3):
        act(T.wo[:, b:128:16], T.wo[:, b:128:16], F.Copy, r=["wo"], w=["wo"], scale=-1.0)
        act(T.wf[:, b:128:16], T.bw[:, 16 + b:144:16], F.Copy, r=["bw", "wf"], w=["wf%d" % b], scale=128.0)

    I, B, Bha, Iah = T.iw[:, 0:128], T.bw[:, 0:128], T.bw[:, 112:240], T.iw[:, 16:144]
    Up, Nf, Ep = pb[6][:, 0:64], pb[6][:, 64:128], pb[6][:, 128:192]
    Ap, Er = pb[7][:, 0:64], pb[7][:, 128:192]
    MK, Y3 = ["mk0", "mk1"], ["y30", "y31"]

    def half(b, wt, src, first, final, r):
        mm([(pb[b][:], wt, src, first, final)], 512, r, ["b%d" % b])

    for t in range(RO):
        last = t == RO - 1
        rg = t % 2
        S0 = BASE + K * rg
        ml, ac = T["ml%d" % t], T["ac%d" % (t % 3)]
        R = [slice(S0, S0 + 512), slice(S0 + 512, S0 + K)]
        win, keys = (T.raw, RAWK) if t == 0 else (T.tab, TABK)
        act(T.p1[:], T.part[:, 0:W].indirect(T.noff[:, 0:64]), F.Copy, 2 * GA - 64, r=PARK + ["noff"], w=["p1"])
        extract(Up, T.zp, 128, T.p1, True, True, ["zp", "p1"], ["b6"])
        ts(T.n1off[:], Up, UPC, None, A.add, w=["n1off"], x=["b6"])
        act(T.dsn[:], Up, F.Identity, w=["dsn"], x=["b6"], bias=UPC - S0)
        mm([(Er, T.iwf[:, 112:240], T.eh[:], True, True)], 256, ["iwf", "eh"], ["b7"])
        cp(T.eoff[:], Er, w=["eoff"], x=["b7"])
        for h in range(2):
            b, hs = ["b%d" % (2 + h)], str(h)
            tt(T.y1[:, H[h]], win[:, 0:W].indirect(T.noff[:, L[h]]), T.x[:, H[h]], A.mult, GA, r=keys + ["noff", "x" + hs], w=["y1" + hs])
            half(2 + h, B, T.y1[:, H[h]], True, True, ["bw", "y1" + hs])
            act(T.xx[:, H[h]], pb[2 + h][:], F.Abs, 512, r=["nb", "nb0"], w=["xx" + hs], x=b, scale=128.0,
                bias=col["nb0" if t == 0 else "nb"])
            half(2 + h, T.bx[:], T.xx[:, H[h]], True, False, ["bx", "xx" + hs])
            tt(T.y2[:, H[h]], T.tab[:, 0:W].indirect(T.n1off[:, L[h]]), T.xx[:, H[h]], A.max, GA,
               r=TABK + ["n1off", "xx" + hs], w=["y2" + hs])
            half(2 + h, Bha, T.y2[:, H[h]], False, True, ["bw", "y2" + hs])
        for h in range(2):
            hs = str(h)
            act(T.z[:, H[h]], ml[:, 0:K].indirect(T.eoff[:, L[h]]), F.Identity, GA,
                r=["ml%d0" % t, "ml%d1" % t, "eoff"], w=["z" + hs], bias=HOLE[t])
            tt(T.mk[:, H[h]], pb[2 + h][:], T.z[:, H[h]], A.is_equal, 512, r=["z" + hs], w=["mk" + hs], x=["b%d" % (2 + h)])
        if not last:
            for h in range(2):
                hs, tk, qk = str(h), "t%d%d" % (rg, h), "q%d%d" % (rg, h)
                half(h, Iah, T.z[:, H[h]], True, False, ["iw", "z" + hs])
                half(h, T.bm[:], T.mk[:, H[h]], False, True, ["bm", "mk" + hs])
                act(T.aa[:, H[h]], pb[h][:], F.Identity, 512, w=["aa" + hs], x=["b" + hs], bias=64.0)
                half(6 + h, I, T.tab[:, R[h]], True, False, ["iw", tk] + TC)
                half(6 + h, T.bp[:], T.mk[:, H[h]], False, True, ["bp", "mk" + hs])
                tt(T.tab[:, R[h]], pb[6 + h][:], T.aa[:, H[h]], A.min, 512, r=["aa" + hs], w=[tk], x=["b%d" % (6 + h)])
                half(4 + h, T.wo[:], T.part[:, R[h]], True, False, ["wo", qk] + PD)
                half(4 + h, T.ws[:], T.p1[:, H[h]], False, False, ["ws", "p1"])
                half(4 + h, T.wf[:], T.mk[:, H[h]], False, True, ["wf1", "wf3", "mk" + hs])
                act(T.part[:, R[h]], pb[4 + h][:], F.Abs, 512, r=["pbias"], w=[qk], x=["b%d" % (4 + h)], bias=col["pb"])
                half(h, T.xw[:], T.mk[:, H[h]], True, True, ["xw", "mk" + hs])
                tt(T.x[:, H[h]], pb[h][:], T.x[:, H[h]], A.is_lt, 512, r=["x" + hs], w=["x" + hs], x=["b" + hs])
            for h in range(2):
                mtab(t + 1, h)
            if t < 2:
                hand_on(t + 1)
                ac_arrives(t + 1, PLAN["push"])
        else:
            extract(pb[4][:, 0:64], T.zr, 128, T.x, True, True, ["zr", "x0", "x1"], ["b4"], block=True)
            act(T.ub[:], pb[4][:, 0:64], F.Copy, w=["ub"], x=["b4"])
            extract(pb[5][:, 0:64], T.zk, 16, T.mk, True, True, ["zk"] + MK, ["b5"], block=True)
            tt(T.um[:], pb[5][:, 0:64], T.ub[:], A.max, r=["ub"], w=["um"], x=["b5"])
            ts(T.us[:], T.um[:], 15, None, A.bitwise_and, r=["um"], w=["us"])
            cp(T.finu[:], T.us[:], r=["us"], w=["finu"])
            dma("s", "yu", T.yu[:], T.finu[:], 32, r=["finu"])
        for h in range(2):
            tt(T.y3[:, H[h]], ac[:, 0:K].indirect(T.eoff[:, L[h]]), T.mk[:, H[h]], A.mult, GA,
               r=ACK[t % 3] + ["eoff", "mk%d" % h], w=["y3%d" % h])
        mm([(Nf, I, T.one[:, 0:64], True, False)], 64, ["iw", "one"], ["b6"])
        extract(Nf, T.zn, 16, T.mk, False, True, ["zn"] + MK, ["b6"])
        tt(T.tq[:], Nf, T.dsn[:], A.mult, r=["dsn"], w=["tq"], x=["b6"])
        tt(T.te[:], Nf, T.eh[:], A.mult, r=["eh"], w=["te"], x=["b6"])
        mm([(Ap, T.iwf[:, 0:128], T.tq[:], True, False)], 256, ["iwf", "tq"], ["b7"])
        extract(Ap, T.zw, 16, T.y3, False, True, ["zw"] + Y3, ["b7"])
        if not last:
            ts(T.noff[:], Ap, float(S0), None, A.add, w=["noff"], x=["b7"])
            mm([(Ep, I, T.te[:], True, False)], 64, ["iw", "te"], ["b6"])
            extract(Ep, T.zw, 16, T.y3, False, True, ["zw"] + Y3, ["b6"])
            act(T.eh[:], Ep, F.Copy, w=["eh"], x=["b6"])
        else:
            tt(T.td[:], T.te[:], T.tq[:], A.subtract, 128, r=["te", "tq"], w=["td"])
            ts(T.finn[:], Ap, float(S0), None, A.add, w=["finn"], x=["b7"])
            dma("y", "yn", T.yn[:], T.finn[:], 32, r=["finn"])
            tt(T.fine[:], Ap, T.td[:], A.add, r=["td"], w=["fine"], x=["b7"])
            dma("s", "ye", T.ye[:], T.fine[:], 32, r=["fine"])

    Q = {"v": g.vector, "s": g.scalar, "p": g.tensor, "g": g, "y": g.sync}
    total = {}
    known = {e: {} for e in Q}
    token = {}
    before = hazards(calls)
    for i in issue_order(calls):
        c = calls[i]
        e = c["e"]
        if e == "dma":
            token[i] = token[i - 1]
            continue
        if e == "-":
            total[c["sem"][0]] = c["sem"][1]
            token[i] = (c["sem"][0], c["sem"][1], {})
            continue
        toks = [token[j] for j in before[i] if j in token and not (e == "p" and calls[j]["e"] == "p")
                and not (c["chain"] and c["chain"] == calls[j]["chain"] and not set(calls[j]["w"]) & set(c["r"] + c["w"]))]
        for sem, val, clock in sorted(toks, key=lambda tk: -tk[1]):
            if known[e].get(sem, 0) < val:
                Q[e].wait_ge(T.sem[sem], val)
                known[e][sem] = val
            for s, v in clock.items():
                known[e][s] = max(known[e].get(s, 0), v)
        ins = c["fn"]()
        if isinstance(c["sem"], tuple):
            total["ls"] = total.get("ls", 0) + c["sem"][1]
            continue
        step = 16 if c["sem"][0] == "d" else 1
        total[c["sem"]] = total.get(c["sem"], 0) + step
        ins.then_inc(T.sem[c["sem"]], step)
        token[i] = (c["sem"], total[c["sem"]], dict(known[e]))
    for s, v in total.items():
        if known["g"].get(s, 0) < v:
            g.wait_ge(T.sem[s], v)
